import numpy as np, ml_dtypes
CORES = [10,34,74,98]
N = 4
import mx_ref
BF = ml_dtypes.bfloat16
def pick(q, e):
    c = np.concatenate([q[0].reshape(128, -1, 4), np.zeros((128, 1, 4), np.uint8)], axis=1); s = np.concatenate([q[1], np.ones((16, 1), np.uint8)], axis=1)
    return (np.ascontiguousarray(c[:, e].reshape(128, -1)), np.ascontiguousarray(s[:, e]))
def join(*qs):
    return (np.concatenate([q[0] for q in qs], axis=1), np.concatenate([q[1] for q in qs], axis=1))
def put(q, e, v):
    c, s = q[0].reshape(128, -1, 4).copy(), q[1].copy(); c[:, e] = v[0].reshape(128, -1, 4); s[:, e] = v[1]
    return (c.reshape(128, -1), s)
def pk(c, s):
    return (np.ascontiguousarray(c), mx_ref.live(s))
def emit(q):
    return q[0], q[1]
def cols(t, e):
    v = np.concatenate([t.reshape(128, -1, 4), np.zeros((128, 1, 4), BF)], axis=1)
    return np.ascontiguousarray(v[:, e]).reshape(128, -1)
def tile(rs):
    return np.stack(rs, axis=2).reshape(128, -1).astype(BF)
def cut(t, i, w=512):
    return t[:, w * i:w * i + w]
def f(rng, *shape):
    return mx_ref.flush((rng.standard_normal(shape, dtype=np.float32) * np.exp2(rng.integers(-2, 3, shape[:-1] + (1,)))).astype(BF))
def wide(rng, *shape, cols=0):
    v = rng.standard_normal(shape, dtype=np.float32) * np.exp2(rng.integers(-12, 13, shape)).astype(np.float32)
    if cols: v *= np.repeat(np.exp2(rng.integers(-cols, cols + 1, shape[:-2] + (1, shape[-1] // 4))) * (rng.random(shape[:-2] + (1, shape[-1] // 4)) > 0.0625), 4, axis=-1).astype(np.float32)
    return mx_ref.flush(v.astype(BF))
P, K, O = 256, 64, 1
E = P + 2 * K // N
def play(x, u, a, b):
    row = mx_ref.quantize(np.concatenate([x[r] for r in range(N)], axis=1))
    num = 4 * np.arange(N * P)
    k = mx_ref.quantize(np.ascontiguousarray(u[0]))
    high = []
    for t in range(2):
        n = num.size
        s = mx_ref.matmul(k, row)[0] + np.float32(0)
        split = np.sort(np.argsort(-s, kind="stable")[:K])
        parents = pick(row, split)
        kids = []
        for m in (a[0], b[0]):
            kids.append(tile([mx_ref.matmul(mx_ref.quantize(np.ascontiguousarray(cut(m, i))), parents) * np.float32(0.0625) for i in range(4)]))
        size = np.max(np.abs(np.stack(kids).astype(np.float32)).reshape(2, 16, 8, K, 4), axis=(2, 4))
        high.append((np.max(np.abs(s)), np.max(size), np.min(np.where(size == 0, np.float32(1), size))))
        e = np.repeat(np.arange(n), 1 + np.isin(np.arange(n), split))
        first = split + np.arange(K)
        num = num[e]
        num[first + 1] += 2 - t
        e[first] = n + np.arange(K)
        e[first + 1] = n + K + np.arange(K)
        row = pick(join(row, mx_ref.quantize(kids[0]), mx_ref.quantize(kids[1])), e)
    return row, num, high
def times(t, v):
    return mx_ref.flush((t.astype(np.float32) * np.float32(v)).astype(BF))
def lift(d, r, e, v):
    s = np.where(d["u"][0][:, None, :4].astype(np.float32) < 0, -v, v)
    x = np.array(d["x"][r].astype(np.float32)).reshape(128, P, 4)
    x[:, e] = np.abs(x[:, e]) * s
    d["x"][r] = mx_ref.flush(x.reshape(128, -1).astype(BF))
def setup_inputs(rng):
    u = np.array(f(rng, 128, 512))
    u[:, 4:] = 0
    return {"x": np.array(f(rng, N, 128, 4 * P)), "u": np.stack([u] * N), "a": np.stack([f(rng, 128, 2048)] * N), "b": np.stack([f(rng, 128, 2048)] * N), "w": f(rng, N, 128, 512 * O)}
def setup_inputs_below(rng):
    d = setup_inputs(rng)
    d["x"] = np.array(times(d["x"], 2.0 ** 20))
    for r in range(N): lift(d, r, np.arange(P), -1)
    lift(d, N - 1, rng.permutation(P)[:K], -2.0 ** -6)
    v, p = d["a"][0].astype(np.float32) * np.float32(2.0 ** -6), np.arange(128)
    for i in range(4): v[p, 512 * i + 4 * p + i] = 128
    d["a"] = np.stack([mx_ref.flush(v.astype(BF))] * N)
    d["b"] = times(d["a"], 2.0 ** -4)
    return d
def setup_inputs_edge(rng):
    d = setup_inputs(rng)
    d["a"], d["b"], d["x"] = times(d["a"], 2.0 ** -12), times(d["b"], 2.0 ** -12), np.array(times(d["x"], 64))
    lift(d, int(rng.integers(1, N - 1)), rng.permutation(P)[:K], 4096)
    lift(d, N - 1, rng.permutation(P)[:K], 64)
    return d
def setup_inputs_spread(rng):
    return {**setup_inputs(rng), "x": wide(rng, N, 128, 4 * P, cols=6)}
def setup_inputs_ties(rng):
    d = setup_inputs(rng)
    v, e = times(f(rng, 128, 24), 2.0 ** 14), (rng.permutation(N * P) % 6).reshape(N, P)
    d["x"] = np.stack([cols(v, e[r]) for r in range(N)])
    lift(d, N - 1, rng.permutation(P)[:K // 8], 64)
    return {**d, "b": d["a"].copy()}
def setup_inputs_zero(rng):
    d = setup_inputs(rng)
    d["u"][:, 64:] = 0
    for r in range(N):
        kind = rng.permutation(P) % 3
        lift(d, r, np.flatnonzero(kind == 2), -1)
        x = np.array(d["x"][r]).reshape(128, P, 4)
        x[:, kind == 0] = 0
        x[:64, kind == 1] = 0
        d["x"][r] = x.reshape(128, -1)
    return d
def check_inputs(d):
    b = []
    for k in ("x", "u", "a", "b", "w"):
        v = np.abs(d[k].astype(np.float32))
        if not (np.isfinite(v).all() and ((v == 0) | (v >= 2.0 ** -30) & (v <= 2.0 ** 30)).all()): b.append("a value of " + k)
    if (d["u"][:, :, 4:].astype(np.float32) != 0).any(): b.append("u has numbers behind its column 0")
    for k in ("u", "a", "b"):
        v = d[k].astype(np.float32)
        if (v != v[:1]).any(): b.append(k + " differs between ranks")
    if not b:
        try:
            high = play(d["x"], d["u"], d["a"], d["b"])[2]
            if not all(np.isfinite(s) for s, c, m in high): b.append("a score")
            if not all(c <= 2.0 ** 30 and m >= 2.0 ** -30 for s, c, m in high): b.append("a number of a child")
        except Exception:
            b.append("a number of a child")
    return b
def reference(x, u, a, b, w):
    row, num, _ = play(x, u, a, b)
    oc, osc = np.zeros((N, 128, 4 * E), np.uint8), np.zeros((N, 16, E), np.uint8)
    hs, y = np.zeros((N, 1, E), np.float32), np.zeros((N, 128, O * E), np.float32)
    for r in range(N):
        q = pick(row, np.arange(r * E, r * E + E))
        oc[r], osc[r] = emit(q)
        hs[r, 0] = num[r * E:r * E + E]
        for o in range(O):
            y[r, :, o * E:o * E + E] = mx_ref.matmul(mx_ref.quantize(np.ascontiguousarray(cut(w[r], o))), q)
    return {"oc": oc, "osc": osc, "hs": hs, "y": y}

@@ -1,0 +1,538 @@
+from concourse.bass import DstId, RemoteDMATransfer
+from concourse.mybir import dt, AluOpType as Alu, AxisListType, ActivationFunctionType as Act
+
+N, P, K, E = 4, 256, 64, 288
+LEN = (1024, 1088)
+CH = ([(128 * c, 0, 4, c // 2) for c in range(8)],
+      [(0, 0, 4, 0), (128, 0, 4, 0), (256, 0, 4, 1), (384, 0, 4, 1), (512, 0, 4, 2), (640, 0, 4, 2), (736, 1, 3, 2), (832, 0, 4, 3), (960, 0, 4, 3)])
+WIN = ([(0, 288), (160, 576), (448, 864), (736, 1024)], [(0, 288), (224, 576), (512, 864), (800, 1088)], [(E * r, E * r + E) for r in range(N)])
+NEED = ([(0, 288), (0, 576), (448, 1024), (736, 1024)], [(0, 288), (0, 576), (512, 1088), (800, 1088)])
+F32, BF, I32, U16 = "float32", "bfloat16", "int32", "uint16"
+SW = 130
+CW = 132
+PAD = 64
+NV = (6, 3)
+CMPW = 448
+
+SCRATCH = {
+    "xt": ("sbuf", [128, 1024], BF), "uin": ("sbuf", [128, 8], BF), "ut": ("sbuf", [128, 512], BF), "uz": ("sbuf", [128, 128], BF),
+    "at": ("sbuf", [128, 2048], BF), "bt": ("sbuf", [128, 2048], BF), "wt": ("sbuf", [128, 512], BF),
+    "msp": ("sbuf", [128, 640], BF), "mrep": ("sbuf", [128, 640], BF), "carb": ("sbuf", [128, 640], BF),
+    "pi": ("sbuf", [128, 4], I32), "dcol": ("sbuf", [128, 2], F32),
+    "psc": ("psum", [128, 2048], F32), "pch": ("psum", [128, 2048], F32),
+    "ysb": ("sbuf", [128, 288], F32), "hsr": ("sbuf", [128, 288], F32),
+    "tn0": ("sbuf", [128, 1248], F32), "tn1": ("sbuf", [128, 1056], F32),
+}
+for _q, _n in (("u", 128), ("a", 512), ("b", 512), ("w", 128), ("r0", 1248), ("r1", 1056), ("r2", 288)):
+    SCRATCH[_q + "c"] = ("sbuf", [128, _n], "float8_e4m3fn_x4")
+    SCRATCH[_q + "s"] = ("sbuf", [128, _n], "uint8")
+for _t in range(2):
+    for _n, _w, _d in (("ha", 1664, BF), ("hb", 1664, BF), ("own", 4, F32), ("land", 8, F32), ("cmp", 9 * CMPW, BF),
+                       ("eq", 384, BF), ("sg", 3 * 320, BF), ("sj", 3 * 320, BF), ("so", 9 * CMPW // 2, BF), ("acc", 3, F32),
+                       ("pland", 16, BF), ("rho", 15, F32), ("mrow", 640, BF), ("inc", 704, BF), ("fb", 752, BF),
+                       ("jt", 18, F32), ("jj", 12, F32), ("xc", 1, F32), ("ch", 6 * CW, BF), ("fs", 6 * CW, BF), ("cu", 1 + 6 * CW // 2, F32),
+                       ("sm", 6, F32), ("qi", 6, I32), ("ws", 6, F32), ("wy", 6, F32), ("ll", 6, F32), ("wf", 24, F32), ("wu", 24, U16)):
+        SCRATCH["%s%d" % (_n, _t)] = ("sbuf", [128, _w], _d)
+SEMAPHORES = ["v", "s", "p", "gc", "sent", "arrw", "dx0", "dx1", "du", "da", "db", "dw", "out"] + ["%s%d_%d" % (k, t, r) for k in ("arr", "cnt") for t in range(2) for r in range(N)]
+
+
+def rank_program(g, core, T, topo):
+    r = T.rank_of(core)
+    if r is None:
+        return
+    Q = {"v": g.vector, "s": g.scalar, "p": g.tensor, "g": g, "y": g.sync}
+    ESEM = {"v": "v", "s": "s", "p": "p", "g": "gc"}
+    total, known, hist = {}, {q: {} for q in Q}, {}
+
+    def V(name, c0=0, c1=None, step=1, p0=0, p1=128):
+        if c1 is None:
+            c1 = SCRATCH[name][1][1]
+        ap = T[name][p0:p1, c0:c1] if step == 1 else T[name][p0:p1, c0:c1:step]
+        return (ap, name, c0, c1, step, p0, p1)
+
+    def clash(x, y):
+        if SCRATCH[x[1]][0] == "psum":
+            return x[2] // 512 <= (y[3] - 1) // 512 and y[2] // 512 <= (x[3] - 1) // 512
+        if x[6] <= y[5] or y[6] <= x[5] or x[3] <= y[2] or y[3] <= x[2]:
+            return False
+        return not (x[4] == y[4] and x[4] > 1 and (x[2] - y[2]) % x[4] != 0)
+
+    def need(q, reads, writes):
+        todo = {}
+        for acc, wr in [(a, False) for a in reads] + [(a, True) for a in writes]:
+            psum = SCRATCH[acc[1]][0] == "psum"
+            for old, owr, s, n, clock, oq in hist.get(acc[1], []):
+                if not (wr or owr or (psum and oq != q)) or known[q].get(s, 0) >= n or not clash(acc, old):
+                    continue
+                if s not in todo or todo[s][0] < n:
+                    todo[s] = (n, clock)
+        for s in sorted(todo):
+            n, clock = todo[s]
+            if known[q].get(s, 0) < n:
+                Q[q].wait_ge(T.sem[s], n)
+                known[q][s] = n
+                for s2, n2 in clock.items():
+                    known[q][s2] = max(known[q].get(s2, 0), n2)
+
+    def note(q, reads, writes, s, n):
+        clock = dict(known[q])
+        for acc, wr in [(a, False) for a in reads] + [(a, True) for a in writes]:
+            hist.setdefault(acc[1], []).append((acc, wr, s, n, clock, q))
+
+    def op(q, call, reads, writes):
+        need(q, reads, writes)
+        s = ESEM[q]
+        total[s] = total.get(s, 0) + 1
+        call().then_inc(T.sem[s], 1)
+        note(q, reads, writes, s, total[s])
+
+    def dma(q, out, in_, sem, reads, writes):
+        need(q, reads, writes)
+        total[sem] = total.get(sem, 0) + 16
+        Q[q].dma_start(out, in_).then_inc(T.sem[sem], 16)
+        note(q, reads, writes, sem, total[sem])
+
+    def sc(x):
+        return x[0] if isinstance(x, tuple) else x
+
+    def ts(out, in0, s1, s2, op0, op1=None):
+        rd = [x for x in (in0, s1, s2) if isinstance(x, tuple)]
+        if op1 is None:
+            op("v", lambda: g.vector.tensor_scalar(out[0], in0[0], sc(s1), None, op0), rd, [out])
+        else:
+            op("v", lambda: g.vector.tensor_scalar(out[0], in0[0], sc(s1), sc(s2), op0, op1), rd, [out])
+
+    def tt(out, a, b, o):
+        op("v", lambda: g.vector.tensor_tensor(out[0], a[0], b[0], o), [a, b], [out])
+
+    def copy(q, out, in_):
+        if q == "v":
+            op("v", lambda: g.vector.tensor_copy(out[0], in_[0]), [in_], [out])
+        else:
+            op("s", lambda: g.scalar.activation(out[0], in_[0], Act.Copy), [in_], [out])
+
+    def act(out, in_, f, bias=0.0, scale=1.0, accum=None):
+        rd = [in_] + [x for x in (bias, scale) if isinstance(x, tuple)]
+        if accum is None:
+            op("s", lambda: g.scalar.activation(out[0], in_[0], f, bias=sc(bias), scale=sc(scale)), rd, [out])
+        else:
+            op("s", lambda: g.scalar.activation(out[0], in_[0], f, bias=sc(bias), scale=sc(scale), accum_out=accum[0]), rd, [out, accum])
+
+    def scan(out, a, b, initial, o0, o1):
+        op("v", lambda: g.vector.tensor_tensor_scan(out[0], a[0], b[0], initial, o0, o1), [a, b], [out])
+
+    def turn(out, in_):
+        op("v", lambda: g.vector.transpose(out[0], in_[0]), [in_], [out])
+
+    def fill(out, c):
+        op("v", lambda: g.vector.memset(out[0], c), [], [out])
+
+    def quant(q, a, b, in_):
+        c, s = V(q + "c", a, b), V(q + "s", a, b)
+        op("v", lambda: g.vector.quantize_mx(c[0], s[0], in_[0]), [in_], [c, s])
+
+    def mm(bank, q1, a1, q2, a2, n):
+        o = V(bank[0], 512 * bank[1], 512 * bank[1] + n)
+        w, ws, x, xs = V(q1 + "c", a1, a1 + 128), V(q1 + "s", a1, a1 + 128), V(q2 + "c", a2, a2 + n), V(q2 + "s", a2, a2 + n)
+        op("p", lambda: g.tensor.matmul_mx(o[0], w[0], ws[0], x[0], xs[0], True, True), [w, ws, x, xs], [o])
+        return o
+
+    def dst(c):
+        rid, pid = topo.addr(c)[:2]
+        return DstId(rid=rid, pnc=pid)
+
+    def engines(cs):
+        return sorted(set.intersection(*[set(topo.engines(core, c)) for c in cs]))
+
+    def send(outs, src, cs, sem):
+        e = engines(cs)
+        need("g", [src], [])
+        g.remote_dma_fused([RemoteDMATransfer(dst_ids=[dst(c) for c in cs], dma_engine_mask=sum(1 << k for k in e), remote_sem=T.sem[sem],
+                                              srcs=[src[0]], dsts=outs)], local_sem=T.sem.sent)
+        total["sent"] = total.get("sent", 0) + len(e)
+
+    def arrive(sem, n, views):
+        total[sem] = total.get(sem, 0) + n
+        for v in views:
+            hist.setdefault(v[1], []).append((v, True, sem, total[sem], {}, None))
+
+    def codes(name, a, b):
+        return T[name][:, a:b].bitcast(dt.uint8)
+
+    def near(c, d):
+        return topo.same_plane(topo.chip(c), topo.chip(d))
+
+    def targets(c):
+        i = T.rank_of(c)
+        return sorted([d for d in T.cores if d != c], key=lambda d: (near(c, d), (T.rank_of(d) - i) % N))
+
+    NW = [WIN[t][r][1] - WIN[t][r][0] for t in range(3)]
+    C = (NW[0], NW[1], 0)
+    others = targets(core)
+    others_r = [T.rank_of(c) for c in others]
+    ENG = len(engines(others))
+    half = (T.cores[:N // 2], T.cores[N // 2:])
+
+    def slot(me, s):
+        return s if s < me else s - 1
+
+    def group(me, t):
+        return list(range(5)) if me < N // 2 else list(range(len(CH[t]) - 5, len(CH[t])))
+
+    def landpos(me, t):
+        return {k: i for i, k in enumerate([k for k, c in enumerate(CH[t]) if c[3] != me])}
+
+    for i in range(2):
+        dma("y", T.xt[:, 512 * i:512 * i + 512], T.x[:, 512 * i:512 * i + 512], "dx%d" % i, [], [V("xt", 512 * i, 512 * i + 512)])
+    dma("s", T.uin[:, 0:4], T.u[:, 0:4], "du", [], [V("uin", 0, 4)])
+    dma("y", T.at[:], T.a[:], "da", [], [V("at")])
+    dma("y", T.bt[:], T.b[:], "db", [], [V("bt")])
+    dma("y", T.wt[:], T.w[:], "dw", [], [V("wt")])
+
+    own0 = (P * r - WIN[0][r][0], P * r - WIN[0][r][0] + P)
+    nb = [s for s in (r - 1, r + 1) if 0 <= s < N]
+    wviews = []
+    for s in nb:
+        a, b = (0, own0[0]) if s < r else (own0[1], NW[0])
+        wviews += [V("r0c", C[0] + a, C[0] + b), V("r0s", C[0] + a, C[0] + b)]
+    arrive("arrw", 2 * ENG * len(nb), wviews)
+    for t in range(2):
+        for s in others_r:
+            cols = [landpos(r, t)[k] for k, c in enumerate(CH[t]) if c[3] == s]
+            arrive("arr%d_%d" % (t, s), ENG, [V("land%d" % t, cols[0], cols[-1] + 1)])
+            arrive("cnt%d_%d" % (t, s), ENG, [V("pland%d" % t, 5 * slot(r, s), 5 * slot(r, s) + 5)])
+
+    plan = []
+    for t in range(2):
+        a, b = NEED[t][r]
+        chunks = [k for k, c in enumerate(CH[t]) if c[0] + 32 * c[2] > a and c[0] + 32 * c[1] < b]
+        back = a > 0
+        end = WIN[t][r][1]
+        lo1, hi1 = WIN[t + 1][r]
+        mid = (lo1 + end) // 2 if back else (lo1 + hi1) // 2
+        plan.append((chunks, a, b - a, back, end, mid, (hi1 - lo1 + 63) // 64))
+
+    def runs(chs, base, size):
+        out = []
+        for i, c in enumerate(chs):
+            lo, hi = max(c[0] + 32 * c[1], base), min(c[0] + 32 * c[2], base + size)
+            x, y, w = 128 * i + lo - c[0], lo - base, hi - lo
+            if out and out[-1][0] + out[-1][2] == x and out[-1][1] + out[-1][2] == y:
+                out[-1] = (out[-1][0], out[-1][1], out[-1][2] + w)
+            else:
+                out.append((x, y, w))
+        return out
+
+    def slice_of(t, i):
+        c = WIN[t + 1][r][0] + 64 * i - 64 - plan[t][1] + PAD
+        return c, c + SW
+
+    fill(V("uz"), 0.0)
+    op("g", lambda: g.iota(T.pi[:, 0:1], [[0, 1]], 0, 1), [], [V("pi", 0, 1)])
+    for t in range(2):
+        e = -1 - K - plan[t][4] if plan[t][3] else -1 - plan[t][5]
+        op("g", lambda: g.iota(T["jt%d" % t][:, 0:6], [[64, 6]], WIN[t + 1][r][0] + e, 1, allow_small_or_imprecise_dtypes=True), [], [V("jt%d" % t, 0, 6)])
+    op("v", lambda: g.vector.tensor_scalar(T.pi[:, 1:2], T.pi[:, 0:1], 96, None, Alu.bitwise_and), [V("pi", 0, 1)], [V("pi", 1, 2)])
+    op("v", lambda: g.vector.tensor_scalar(T.pi[:, 2:3], T.pi[:, 0:1], 16, None, Alu.bitwise_and), [V("pi", 0, 1)], [V("pi", 2, 3)])
+    ts(V("dcol", 0, 1), V("pi", 1, 2), -1.0, None, Alu.mult)
+    ts(V("dcol", 1, 2), V("pi", 2, 3), -2.0, V("dcol", 0, 1), Alu.mult, Alu.add)
+    fill(V("msp"), 0.0)
+    fill(V("carb"), 1.0)
+    fill(V("carb", 0, 640, 32), 0.0)
+
+    def steps(t):
+        chunks, first, n, back, end, mid, m = plan[t]
+        for x, y, w in runs([CH[t][k] for k in chunks], first, n):
+            odd = x // 32 % 2
+            n2 = (w + 63) // 64
+            op("g", lambda: g.iota(T["inc%d" % t][:, y:y + 64 * n2], [[0, n2], [1 - 2 * odd, 2], [0, 32]], 2 + odd, 0, allow_small_or_imprecise_dtypes=True),
+               [], [V("inc%d" % t, y, y + 64 * n2)])
+
+    def last_steps(t):
+        chunks, first, n, back, end, mid, m = plan[t]
+        x, y, w = runs([CH[t][k] for k in chunks], first, n)[-1]
+        last = 2 + (x + w - 32) // 32 % 2
+        far = 2 * (first + n - end)
+        if far:
+            fill(V("inc%d" % t, n - 1, n), float(last - 256))
+            fill(V("inc%d" % t, n - 2, n - 1), float(last - (far - 256)))
+
+    def tables(t):
+        chunks, first, n, back, end, mid, m = plan[t]
+        fb, lo1 = "fb%d" % t, WIN[t + 1][r][0]
+
+        def put(out, c):
+            act(out, V("uz", 0, out[3] - out[2]), Act.Identity, bias=float(c))
+        put(V(fb, PAD, PAD + 1), 2 * (first - mid))
+        if slice_of(t, 0)[0] < PAD:
+            put(V(fb, 0, PAD), -600)
+        z = slice_of(t, m - 1)[1]
+        if z > PAD + n + 1:
+            put(V(fb, PAD + n + 1, z), 600)
+        put(V("cu%d" % t, 0, 1), 0)
+        for i in range(m):
+            k = -(i * (128 * SW + 384) + 6 * (lo1 - 64 - WIN[t][r][0]) - 6)
+            hi = (k // 512) * 512
+            put(V("ch%d" % t, CW * i + SW, CW * i + SW + 1), hi)
+            put(V("ch%d" % t, CW * i + SW + 1, CW * i + CW), k - hi)
+        act(V("jt%d" % t, 6, 12), V("jt%d" % t, 0, 6), Act.Identity, bias=V("dcol", 1, 2), scale=2.0)
+        act(V("jt%d" % t, 12, 18), V("jt%d" % t, 6, 12), Act.Identity, bias=6.0)
+        if not back:
+            act(V("xc%d" % t), V("jt%d" % t, 12, 13), Act.Copy, scale=float(SW))
+
+    steps(0)
+    tables(0)
+    tables(1)
+    for k in range(4):
+        ts(V("ut", k, 512, 4), V("uz"), V("uin", k, k + 1), None, Alu.add)
+    quant("u", 0, 128, V("ut"))
+    for i in range(2):
+        quant("r0", C[0] + own0[0] + 128 * i, C[0] + own0[0] + 128 * i + 128, V("xt", 512 * i, 512 * i + 512))
+
+    def score(t):
+        q = "r%d" % t
+        w0 = WIN[t][r][0] - C[t]
+        mine = [c for c in CH[t] if c[3] == r]
+        n = len(mine)
+        for i, c in enumerate(mine):
+            mm(("psc", 1 + i), q, c[0] - w0, "u", 0, 128)
+        lo, hi = mine[0][0] + 32 * mine[0][1], mine[-1][0] + 32 * mine[-1][2]
+        mm(("psc", 0), "u", 0, q, lo - w0, hi - lo)
+        mm(("pch", 3), "u", 0, q, lo - w0, hi - lo)
+        ow = V("own%d" % t, 0, n)
+        copy("v", ow, V("psc", 512, 512 * n + 1, 512))
+        outs = []
+        for c in others:
+            p = landpos(T.rank_of(c), t)[CH[t].index(mine[0])]
+            outs.append(T["land%d" % t][:, p:p + n])
+        send(outs, ow, others, "arr%d_%d" % (t, r))
+
+    score(0)
+    for s in nb:
+        sw = WIN[0][s]
+        lo, hi = max(P * r, sw[0]), min(P * r + P, sw[1])
+        a, b = lo - WIN[0][r][0] + C[0], hi - WIN[0][r][0] + C[0]
+        e = sw[1] - sw[0] - sw[0]
+        c, d = lo + e, hi + e
+        send([codes("r0c", c, d)], (codes("r0c", a, b),) + V("r0c", a, b)[1:], [T.cores[s]], "arrw")
+        send([T.r0s[:, c:d]], V("r0s", a, b), [T.cores[s]], "arrw")
+    bank = [0]
+
+    def kids(t, qs, part, cols=None):
+        q, w = "r%d" % t, NW[t]
+        lo, hi = cols or (0, w)
+        m0 = max(0, min(lo, hi - 128))
+        n = max(hi, m0 + 128) - m0
+        for i in part:
+            buf, k = (("pch", 0), ("pch", 1), ("pch", 2), ("psc", 1), ("psc", 2), ("psc", 3))[bank[0] % 6]
+            bank[0] += 1
+            mm((buf, k), "ab"[i // 4], 128 * (i % 4), q, C[t] + m0, n)
+            o = V(buf, 512 * k + lo - m0, 512 * k + hi - m0)
+            h = V("h%s%d" % ("ab"[i // 4], t), 4 * lo + i % 4, 4 * hi, 4)
+            if qs[i] == "v":
+                ts(h, o, 0.0625, None, Alu.mult)
+            else:
+                act(h, o, Act.Copy, scale=0.0625)
+
+    def kidq(t, pieces):
+        q, w = "r%d" % t, NW[t]
+        return [p and (lambda k=p[0], x=p[1], y=p[2]: quant(q, 2 * k * w + x, 2 * k * w + y, V("h%s%d" % ("ab"[k], t), 4 * x, 4 * y))) for p in pieces]
+
+    def fillin(jobs):
+        job = jobs.pop(0) if jobs else None
+        if job:
+            job()
+
+    def order(t, flight1, flight2, hook2, jobs):
+        chunks, first, n, back, end, mid, m = plan[t]
+        lp = landpos(r, t)
+        land, so, z = "land%d" % t, "so%d" % t, CMPW // 2
+        chunks_of = [[k for k, c in enumerate(CH[t]) if c[3] == s] for s in range(N)]
+        mine = chunks_of[r]
+        lo = CH[t][mine[0]][0] + 32 * CH[t][mine[0]][1]
+        hi = CH[t][mine[-1]][0] + 32 * CH[t][mine[-1]][2]
+        W = hi - lo
+
+        def row(a, b):
+            return V("psc", a - lo, b - lo)
+
+        def total_of(k, w):
+            x, y = CMPW * k, w // 2
+            scan(V(so, 9 * (z - y) + k, 9 * (z - 1) + k + 1, 9), V("cmp%d" % t, x, x + y), V("cmp%d" % t, x + y, x + w), 0.0, Alu.add, Alu.add)
+
+        def part(k, m=1):
+            return V(so, 9 * (z - 1) + k, 9 * (z - 1) + k + m, 9 if m == 1 else 1)
+
+        wide = {}
+        for i, k in enumerate(mine):
+            s = CH[t][k][0]
+            e = min(s + 128, hi)
+            val = V("own%d" % t, i, i + 1)
+            x = CMPW * k
+            q = V("eq%d" % t, 128 * i, 128 * i + e - s)
+            d = V("cmp%d" % t, x + W, x + W + e - s)
+            ts(q, row(s, e), val, None, Alu.is_equal)
+            op("g", lambda: g.affine_select(d[0], q[0], [[-1, e - s]], Alu.is_gt, 0.0, 0, 1), [q], [d])
+            if s > lo:
+                ts(V("cmp%d" % t, x, x + s - lo), row(lo, s), val, None, Alu.is_ge)
+            ts(V("cmp%d" % t, x + s - lo, x + W), row(s, hi), val, None, Alu.is_gt)
+            wide[k] = W + e - s
+        flight1()
+        first_r, second_r, third_r = sorted(others_r, key=lambda s: targets(T.cores[s]).index(core))
+        byS, byV = (third_r, second_r) if len(chunks_of[second_r]) > len(chunks_of[third_r]) else (second_r, third_r)
+        for i, k in enumerate(chunks_of[byS]):
+            act(V("sg%d" % t, 320 * i, 320 * i + W), V("pch", 1536, 1536 + W), Act.Sign, bias=V(land, lp[k], lp[k] + 1), scale=-1.0)
+            act(V("sj%d" % t, 320 * i, 320 * i + W), V("sg%d" % t, 320 * i, 320 * i + W), Act.Relu, scale=1.0 if r < byS else -1.0, accum=V("acc%d" % t, i, i + 1))
+            act(part(k), V("acc%d" % t, i, i + 1), Act.Copy, scale=-1.0 if r < byS else 1.0, bias=float(W) if r < byS else 0.0)
+        last = None
+        for s in (first_r, byV):
+            for k in chunks_of[s]:
+                ts(V("cmp%d" % t, CMPW * k, CMPW * k + W), row(lo, hi), V(land, lp[k], lp[k] + 1), None, Alu.is_ge if r < s else Alu.is_gt)
+                if last is not None:
+                    total_of(last, W)
+                last = k
+        total_of(last, W)
+        for k in mine:
+            total_of(k, wide[k])
+        for h in sorted(half, key=lambda h: core not in h):
+            cs = [c for c in others if c in h]
+            k0 = group(T.rank_of(h[0]), t)[0]
+            send([T["pland%d" % t][:, 5 * slot(T.rank_of(c), r):5 * slot(T.rank_of(c), r) + 5] for c in cs], part(k0, 5), cs, "cnt%d_%d" % (t, r))
+        flight2()
+        k0, nc = chunks[0], len(chunks)
+        o = chunks[0] - group(r, t)[0]
+        at = part(k0, nc)
+        for i, s in enumerate(sorted(others_r, key=lambda s: (s // 2 != r // 2, near(core, T.cores[s])))):
+            to = V("rho%d" % t, 5 * i, 5 * i + nc)
+            tt(to, at, V("pland%d" % t, 5 * slot(r, s) + o, 5 * slot(r, s) + o + nc), Alu.add)
+            at = to
+        for b in range(4):
+            for a in range(4):
+                src = V("rho%d" % t, 10, 10 + nc, 1, 32 * a, 32 * a + 32)
+                to = V("msp", 32 * a, 128 * nc, 128, 32 * b, 32 * b + 32)
+                if a % 2:
+                    act(to, src, Act.Sign, bias=K - 0.5, scale=-1.0)
+                else:
+                    ts(to, src, float(K), 2.0, Alu.is_lt, Alu.mult)
+        hook2()
+        fillin(jobs)
+        pieces = runs([CH[t][k] for k in chunks], first, n)
+        x0, x1 = pieces[0][0], pieces[-1][0] + pieces[-1][2]
+        scan(V("mrep", x0, x1), V("carb", x0, x1), V("msp", x0, x1), 0.0, Alu.mult, Alu.add)
+        fillin(jobs)
+        for x, y, w in pieces:
+            turn(V("mrow%d" % t, y, y + w), V("mrep", x, x + w))
+        fillin(jobs)
+        fb = "fb%d" % t
+        scan(V(fb, PAD + 1, PAD + n + 1), V("mrow%d" % t, 0, n), V("inc%d" % t, 0, n), float(2 * (first - mid)), Alu.add, Alu.add)
+        fillin(jobs)
+        jj, o = "jt%d" % t, 6
+        if back:
+            jj, o = "jj%d" % t, 0
+            ts(V(jj), V("jt%d" % t, 6, 18), V(fb, PAD + n, PAD + n + 1), None, Alu.add)
+            if t == 0:
+                ts(V("xc%d" % t), V(jj, 6, 7), float(SW), None, Alu.mult)
+            else:
+                act(V("xc%d" % t), V(jj, 6, 7), Act.Copy, scale=float(SW))
+        nv = min(m, NV[t])
+        hm = m - nv
+        for i in range(m):
+            x, y = slice_of(t, i)
+            ts(V("ch%d" % t, CW * i, CW * i + SW), V(fb, x, y), V(jj, o + i, o + i + 1), V(jj, o + 6 + i, o + 7 + i), Alu.max, Alu.min)
+            if i < hm:
+                act(V("fs%d" % t, CW * i, CW * i + CW), V("ch%d" % t, CW * i, CW * i + CW), Act.Copy, accum=V("sm%d" % t, i, i + 1))
+        cu, h = "cu%d" % t, CW // 2
+        scan(V(cu, 1, 1 + nv * h), V("ch%d" % t, hm * CW, m * CW, 2), V("ch%d" % t, hm * CW + 1, m * CW, 2), 0.0, Alu.add, Alu.add)
+        fillin(jobs)
+        sm, W = V("sm%d" % t, 0, m), NW[t]
+        tt(V("sm%d" % t, hm, m), V(cu, h, nv * h + 1, h), V(cu, 0, (nv - 1) * h + 1, h), Alu.subtract)
+        ts(V("qi%d" % t, 0, m), sm, V("xc%d" % t), -1.0 / 6, Alu.subtract, Alu.mult)
+        ts(V("ws%d" % t, 0, m), sm, V("xc%d" % t), -0.5 * W, Alu.subtract, Alu.mult)
+        ts(V("wy%d" % t, 0, m), V("qi%d" % t, 0, m), float(1 - 3 * W), float(W), Alu.mult, Alu.add)
+        tt(V("ll%d" % t, 0, m), V("ws%d" % t, 0, m), V("wy%d" % t, 0, m), Alu.add)
+        for b in range(4):
+            for a in range(4):
+                copy("s" if (a + b) % 2 and (a, b) != (0, 1) else "v", V("wf%d" % t, a, 4 * m, 4, 32 * b, 32 * b + 32), V("ll%d" % t, 0, m, 1, 32 * a, 32 * a + 32))
+        while jobs:
+            fillin(jobs)
+        copy("v", V("wu%d" % t, 0, 4 * m), V("wf%d" % t, 0, 4 * m))
+
+    def pick(t, x=0, y=None):
+        y, w = y or NW[t + 1], 3 * NW[t]
+        off = V("wu%d" % t, x // 16, y // 16)
+        a, b = V("r%dc" % t, 0, w), V("r%dc" % (t + 1), C[t + 1] + x, C[t + 1] + y)
+        op("v", lambda: g.vector.tensor_copy(b[0].bitcast(dt.uint32), a[0].bitcast(dt.uint32).indirect(off[0])), [a, off], [b])
+        c, d = V("r%ds" % t, 0, w), V("r%ds" % (t + 1), C[t + 1] + x, C[t + 1] + y)
+        op("s", lambda: g.scalar.activation(d[0], c[0].indirect(off[0]), Act.Copy), [c, off], [d])
+
+    def numbers(t, out):
+        n, w = NW[t + 1], 3 * NW[t]
+        off, a = V("wu%d" % t, 0, n // 16), V("tn%d" % t, 0, w)
+        op("s", lambda: g.scalar.activation(out[0], a[0].indirect(off[0]), Act.Copy), [a, off], [out])
+
+    border = [(0, own0[0])] * (own0[0] > 0) + [(own0[1], NW[0])] * (own0[1] < NW[0])
+    if len(border) == 2:
+        jobs = [(0, 144, 288), None, None, None, None, (1, 0, NW[0]), (0, 0, 144), (0, 288, NW[0])]
+    elif r == 0:
+        jobs = [(0, 0, 144), None, None, None, None, (1, 0, NW[0]), (0, 144, NW[0])]
+    else:
+        jobs = [(0, 144, NW[0]), None, None, None, None, (1, 0, NW[0]), (0, 0, 144)]
+    inner = jobs.pop(0)
+
+    def flight_of_scores0():
+        last_steps(0)
+        quant("a", 0, 512, V("at"))
+
+    def flight_of_counts0():
+        kids(0, "vsvsssss", range(4), own0)
+        quant("b", 0, 512, V("bt"))
+        kidq(0, [inner])[0]()
+        kids(0, "ssssssss", range(4, 5), own0)
+        steps(1)
+        for i in range(3):
+            op("g", lambda: g.iota(T.tn0[:, NW[0] * i:NW[0] * i + NW[0]], [[4, NW[0]]], 4 * WIN[0][r][0] + (2 if i == 2 else 0), 0, allow_small_or_imprecise_dtypes=True),
+               [], [V("tn0", NW[0] * i, NW[0] * i + NW[0])])
+
+    def rest_kids():
+        kids(0, "ssssssss", range(5, 8))
+        for x in border:
+            kids(0, "ssssssss", range(4, 5), x)
+        for x in border:
+            kids(0, "ssssssss", range(4), x)
+    order(0, flight_of_scores0, flight_of_counts0, rest_kids, kidq(0, jobs))
+    pick(0)
+    score(1)
+    bank[0] = 0
+
+    def flight_of_scores1():
+        last_steps(1)
+        kids(1, "sss", range(3))
+        quant("w", 0, 128, V("wt"))
+
+    def flight_of_counts1():
+        kids(1, "ssssvsvs", range(3, 8))
+        for job in kidq(1, [(0, 0, NW[1]), (1, 0, NW[1])]):
+            job()
+
+    def new_numbers():
+        numbers(0, V("tn1", 0, NW[1]))
+        copy("s", V("tn1", NW[1], 2 * NW[1]), V("tn1", 0, NW[1]))
+        act(V("tn1", 2 * NW[1], 3 * NW[1]), V("tn1", 0, NW[1]), Act.Identity, bias=1.0)
+    order(1, flight_of_scores1, flight_of_counts1, new_numbers, [])
+    cut = ((0, 160), (160, E))
+    for x, y in cut:
+        pick(1, x, y)
+    outs = [mm(("psc", i), "w", 0, "r2", x, y - x) for i, (x, y) in enumerate(cut)]
+    numbers(1, V("hsr"))
+
+    for x, y in cut:
+        dma("y", T.oc[:, 4 * x:4 * y], codes("r2c", x, y), "out", [V("r2c", x, y)], [])
+    for k in range(4):
+        dma("y", T.osc[4 * k:4 * k + 4, :], T.r2s[32 * k:32 * k + 4, :], "out", [V("r2s")], [])
+    dma("s", T.hs[:], T.hsr[0:1, :], "out", [V("hsr")], [])
+    for o, (x, y) in zip(outs, cut):
+        copy("v", V("ysb", x, y), o)
+        dma("y", T.y[:, x:y], T.ysb[:, x:y], "out", [V("ysb", x, y)], [])
+    for s in sorted(total):
+        if known["g"].get(s, 0) < total[s]:
+            g.wait_ge(T.sem[s], total[s])

@@ -2,23 +2,24 @@ from concourse.bass import DstId, RemoteDMATransfer
 from concourse.mybir import dt, AluOpType as Alu, AxisListType, ActivationFunctionType as Act
 
 N, P, K, E = 4, 256, 64, 288
-LEN = (1024, 1088)
 CH = ([(128 * c, 0, 4, c // 2) for c in range(8)],
-      [(0, 0, 4, 0), (128, 0, 4, 0), (256, 0, 4, 1), (384, 0, 4, 1), (512, 0, 4, 2), (640, 0, 4, 2), (736, 1, 3, 2), (832, 0, 4, 3), (960, 0, 4, 3)])
+      [(0, 0, 4, 0), (128, 0, 4, 0), (256, 0, 4, 1), (384, 0, 4, 1), (448, 2, 4, 1), (576, 0, 4, 2), (704, 0, 4, 2), (832, 0, 4, 3), (960, 0, 4, 3)])
 WIN = ([(0, 288), (160, 576), (448, 864), (736, 1024)], [(0, 288), (224, 576), (512, 864), (800, 1088)], [(E * r, E * r + E) for r in range(N)])
 NEED = ([(0, 288), (0, 576), (448, 1024), (736, 1024)], [(0, 288), (0, 576), (512, 1088), (800, 1088)])
 F32, BF, I32, U16 = "float32", "bfloat16", "int32", "uint16"
-SW = 130
-CW = 132
-PAD = 64
-NV = (6, 3)
+M = 6
+SW = 81
+CW = 82
+FW = 192
+B0 = 512
 CMPW = 448
 
 SCRATCH = {
     "xt": ("sbuf", [128, 1024], BF), "uin": ("sbuf", [128, 8], BF), "ut": ("sbuf", [128, 512], BF), "uz": ("sbuf", [128, 128], BF),
     "at": ("sbuf", [128, 2048], BF), "bt": ("sbuf", [128, 2048], BF), "wt": ("sbuf", [128, 512], BF),
-    "msp": ("sbuf", [128, 640], BF), "mrep": ("sbuf", [128, 640], BF), "carb": ("sbuf", [128, 640], BF),
-    "pi": ("sbuf", [128, 4], I32), "dcol": ("sbuf", [128, 2], F32),
+    "msp": ("sbuf", [128, B0 + FW], BF), "mrep": ("sbuf", [128, FW], BF), "carb": ("sbuf", [128, FW], BF), "inc": ("sbuf", [128, FW], BF),
+    "cz": ("sbuf", [128, 32], BF), "jt": ("sbuf", [128, 18], F32), "ch": ("sbuf", [128, M * CW], BF), "cu": ("sbuf", [128, 1 + M * CW // 2], F32),
+    "pi": ("sbuf", [128, 4], I32), "dcol": ("sbuf", [128, 3], F32),
     "psc": ("psum", [128, 2048], F32), "pch": ("psum", [128, 2048], F32),
     "ysb": ("sbuf", [128, 288], F32), "hsr": ("sbuf", [128, 288], F32),
     "tn0": ("sbuf", [128, 1248], F32), "tn1": ("sbuf", [128, 1056], F32),
@@ -29,9 +30,8 @@ for _q, _n in (("u", 128), ("a", 512), ("b", 512), ("w", 128), ("r0", 1248), ("r
 for _t in range(2):
     for _n, _w, _d in (("ha", 1664, BF), ("hb", 1664, BF), ("own", 4, F32), ("land", 8, F32), ("cmp", 9 * CMPW, BF),
                        ("eq", 384, BF), ("sg", 3 * 320, BF), ("sj", 3 * 320, BF), ("so", 9 * CMPW // 2, BF), ("acc", 3, F32),
-                       ("pland", 16, BF), ("rho", 15, F32), ("mrow", 640, BF), ("inc", 704, BF), ("fb", 752, BF),
-                       ("jt", 18, F32), ("jj", 12, F32), ("xc", 1, F32), ("ch", 6 * CW, BF), ("fs", 6 * CW, BF), ("cu", 1 + 6 * CW // 2, F32),
-                       ("sm", 6, F32), ("qi", 6, I32), ("ws", 6, F32), ("wy", 6, F32), ("ll", 6, F32), ("wf", 24, F32), ("wu", 24, U16)):
+                       ("pland", 16, BF), ("rho", 15, F32), ("mrow", FW, BF), ("fb", FW, BF), ("mq", 32, BF), ("tot", 1, F32), ("xc", 1, F32),
+                       ("sm", 6, F32), ("qi", 6, I32), ("ws", 6, F32), ("wy", 6, F32), ("wf", 24, F32), ("wu", 24, U16)):
         SCRATCH["%s%d" % (_n, _t)] = ("sbuf", [128, _w], _d)
 SEMAPHORES = ["v", "s", "p", "gc", "sent", "arrw", "dx0", "dx1", "du", "da", "db", "dw", "out"] + ["%s%d_%d" % (k, t, r) for k in ("arr", "cnt") for t in range(2) for r in range(N)]
 
@@ -119,7 +119,8 @@ def rank_program(g, core, T, topo):
             op("s", lambda: g.scalar.activation(out[0], in_[0], f, bias=sc(bias), scale=sc(scale), accum_out=accum[0]), rd, [out, accum])
 
     def scan(out, a, b, initial, o0, o1):
-        op("v", lambda: g.vector.tensor_tensor_scan(out[0], a[0], b[0], initial, o0, o1), [a, b], [out])
+        rd = [x for x in (a, b, initial) if isinstance(x, tuple)]
+        op("v", lambda: g.vector.tensor_tensor_scan(out[0], a[0], b[0], sc(initial), o0, o1), rd, [out])
 
     def turn(out, in_):
         op("v", lambda: g.vector.transpose(out[0], in_[0]), [in_], [out])
@@ -182,7 +183,8 @@ def rank_program(g, core, T, topo):
     def landpos(me, t):
         return {k: i for i, k in enumerate([k for k, c in enumerate(CH[t]) if c[3] != me])}
 
-    for i in range(2):
+    halves = (0, 1) if r else (1, 0)
+    for i in halves:
         dma("y", T.xt[:, 512 * i:512 * i + 512], T.x[:, 512 * i:512 * i + 512], "dx%d" % i, [], [V("xt", 512 * i, 512 * i + 512)])
     dma("s", T.uin[:, 0:4], T.u[:, 0:4], "du", [], [V("uin", 0, 4)])
     dma("y", T.at[:], T.a[:], "da", [], [V("at")])
@@ -206,88 +208,50 @@ def rank_program(g, core, T, topo):
     for t in range(2):
         a, b = NEED[t][r]
         chunks = [k for k, c in enumerate(CH[t]) if c[0] + 32 * c[2] > a and c[0] + 32 * c[1] < b]
-        back = a > 0
-        end = WIN[t][r][1]
-        lo1, hi1 = WIN[t + 1][r]
-        mid = (lo1 + end) // 2 if back else (lo1 + hi1) // 2
-        plan.append((chunks, a, b - a, back, end, mid, (hi1 - lo1 + 63) // 64))
-
-    def runs(chs, base, size):
-        out = []
-        for i, c in enumerate(chs):
-            lo, hi = max(c[0] + 32 * c[1], base), min(c[0] + 32 * c[2], base + size)
-            x, y, w = 128 * i + lo - c[0], lo - base, hi - lo
-            if out and out[-1][0] + out[-1][2] == x and out[-1][1] + out[-1][2] == y:
-                out[-1] = (out[-1][0], out[-1][1], out[-1][2] + w)
-            else:
-                out.append((x, y, w))
-        return out
-
-    def slice_of(t, i):
-        c = WIN[t + 1][r][0] + 64 * i - 64 - plan[t][1] + PAD
-        return c, c + SW
+        plan.append((chunks, a > 0))
 
     fill(V("uz"), 0.0)
     op("g", lambda: g.iota(T.pi[:, 0:1], [[0, 1]], 0, 1), [], [V("pi", 0, 1)])
-    for t in range(2):
-        e = -1 - K - plan[t][4] if plan[t][3] else -1 - plan[t][5]
-        op("g", lambda: g.iota(T["jt%d" % t][:, 0:6], [[64, 6]], WIN[t + 1][r][0] + e, 1, allow_small_or_imprecise_dtypes=True), [], [V("jt%d" % t, 0, 6)])
+    op("g", lambda: g.iota(T.jt[:, 0:M], [[16, M]], -1, 0, allow_small_or_imprecise_dtypes=True), [], [V("jt", 0, M)])
     op("v", lambda: g.vector.tensor_scalar(T.pi[:, 1:2], T.pi[:, 0:1], 96, None, Alu.bitwise_and), [V("pi", 0, 1)], [V("pi", 1, 2)])
-    op("v", lambda: g.vector.tensor_scalar(T.pi[:, 2:3], T.pi[:, 0:1], 16, None, Alu.bitwise_and), [V("pi", 0, 1)], [V("pi", 2, 3)])
-    ts(V("dcol", 0, 1), V("pi", 1, 2), -1.0, None, Alu.mult)
-    ts(V("dcol", 1, 2), V("pi", 2, 3), -2.0, V("dcol", 0, 1), Alu.mult, Alu.add)
-    fill(V("msp"), 0.0)
+    op("v", lambda: g.vector.tensor_scalar(T.pi[:, 2:3], T.pi[:, 0:1], 15, None, Alu.bitwise_and), [V("pi", 0, 1)], [V("pi", 2, 3)])
+    fill(V("msp", B0), 0.0)
     fill(V("carb"), 1.0)
-    fill(V("carb", 0, 640, 32), 0.0)
-
-    def steps(t):
-        chunks, first, n, back, end, mid, m = plan[t]
-        for x, y, w in runs([CH[t][k] for k in chunks], first, n):
-            odd = x // 32 % 2
-            n2 = (w + 63) // 64
-            op("g", lambda: g.iota(T["inc%d" % t][:, y:y + 64 * n2], [[0, n2], [1 - 2 * odd, 2], [0, 32]], 2 + odd, 0, allow_small_or_imprecise_dtypes=True),
-               [], [V("inc%d" % t, y, y + 64 * n2)])
-
-    def last_steps(t):
-        chunks, first, n, back, end, mid, m = plan[t]
-        x, y, w = runs([CH[t][k] for k in chunks], first, n)[-1]
-        last = 2 + (x + w - 32) // 32 % 2
-        far = 2 * (first + n - end)
-        if far:
-            fill(V("inc%d" % t, n - 1, n), float(last - 256))
-            fill(V("inc%d" % t, n - 2, n - 1), float(last - (far - 256)))
-
-    def tables(t):
-        chunks, first, n, back, end, mid, m = plan[t]
-        fb, lo1 = "fb%d" % t, WIN[t + 1][r][0]
-
-        def put(out, c):
-            act(out, V("uz", 0, out[3] - out[2]), Act.Identity, bias=float(c))
-        put(V(fb, PAD, PAD + 1), 2 * (first - mid))
-        if slice_of(t, 0)[0] < PAD:
-            put(V(fb, 0, PAD), -600)
-        z = slice_of(t, m - 1)[1]
-        if z > PAD + n + 1:
-            put(V(fb, PAD + n + 1, z), 600)
-        put(V("cu%d" % t, 0, 1), 0)
-        for i in range(m):
-            k = -(i * (128 * SW + 384) + 6 * (lo1 - 64 - WIN[t][r][0]) - 6)
-            hi = (k // 512) * 512
-            put(V("ch%d" % t, CW * i + SW, CW * i + SW + 1), hi)
-            put(V("ch%d" % t, CW * i + SW + 1, CW * i + CW), k - hi)
-        act(V("jt%d" % t, 6, 12), V("jt%d" % t, 0, 6), Act.Identity, bias=V("dcol", 1, 2), scale=2.0)
-        act(V("jt%d" % t, 12, 18), V("jt%d" % t, 6, 12), Act.Identity, bias=6.0)
-        if not back:
-            act(V("xc%d" % t), V("jt%d" % t, 12, 13), Act.Copy, scale=float(SW))
-
-    steps(0)
-    tables(0)
-    tables(1)
+    fill(V("inc"), 1.0)
+    fill(V("cz"), 1.0)
+    fill(V("cu", 0, 1), 0.0)
+    for t in range(2):
+        fill(V("mq%d" % t), 0.0)
+    ts(V("dcol", 0, 1), V("pi", 2, 3), 1.0, None, Alu.mult)
+    ts(V("dcol", 1, 2), V("pi", 1, 2), 3.0 * 16 * M / 32, None, Alu.mult)
+    fill(V("carb", 0, FW, 32), 0.0)
+    fill(V("inc", 0, 32), 0.0)
+    fill(V("cz", 24, 32), 0.0)
+    act(V("jt", M, 2 * M), V("jt", 0, M), Act.Identity, bias=V("dcol", 0, 1))
+    act(V("jt", 2 * M, 3 * M), V("jt", M, 2 * M), Act.Identity, bias=3.0)
+    act(V("ch", SW, M * CW, CW), V("jt", 0, M), Act.Identity, bias=-3.0 - SW, scale=-3.0 - SW)
+    act(V("dcol", 2, 3), V("dcol", 0, 1), Act.Identity, bias=V("dcol", 1, 2), scale=float(SW))
+    for t in range(2):
+        act(V("xc%d" % t), V("dcol", 2, 3), Act.Identity, bias=float(3 * (WIN[t + 1][r][0] - K - WIN[t][r][0]) + 2 * SW - 3))
     for k in range(4):
         ts(V("ut", k, 512, 4), V("uz"), V("uin", k, k + 1), None, Alu.add)
     quant("u", 0, 128, V("ut"))
-    for i in range(2):
+
+    def border_to(s, plane):
+        sw = WIN[0][s]
+        lo, hi = max(P * r, sw[0]), min(P * r + P, sw[1])
+        a, b = lo - WIN[0][r][0] + C[0], hi - WIN[0][r][0] + C[0]
+        e = sw[1] - sw[0] - sw[0]
+        c, d = lo + e, hi + e
+        if plane:
+            send([T.r0s[:, c:d]], V("r0s", a, b), [T.cores[s]], "arrw")
+        else:
+            send([codes("r0c", c, d)], (codes("r0c", a, b),) + V("r0c", a, b)[1:], [T.cores[s]], "arrw")
+
+    for i in halves:
         quant("r0", C[0] + own0[0] + 128 * i, C[0] + own0[0] + 128 * i + 128, V("xt", 512 * i, 512 * i + 512))
+        if i == halves[0]:
+            border_to(nb[0], True)
 
     def score(t):
         q = "r%d" % t
@@ -309,13 +273,9 @@ def rank_program(g, core, T, topo):
 
     score(0)
     for s in nb:
-        sw = WIN[0][s]
-        lo, hi = max(P * r, sw[0]), min(P * r + P, sw[1])
-        a, b = lo - WIN[0][r][0] + C[0], hi - WIN[0][r][0] + C[0]
-        e = sw[1] - sw[0] - sw[0]
-        c, d = lo + e, hi + e
-        send([codes("r0c", c, d)], (codes("r0c", a, b),) + V("r0c", a, b)[1:], [T.cores[s]], "arrw")
-        send([T.r0s[:, c:d]], V("r0s", a, b), [T.cores[s]], "arrw")
+        border_to(s, False)
+        if s != nb[0]:
+            border_to(s, True)
     bank = [0]
 
     def kids(t, qs, part, cols=None):
@@ -344,7 +304,7 @@ def rank_program(g, core, T, topo):
             job()
 
     def order(t, flight1, flight2, hook2, jobs):
-        chunks, first, n, back, end, mid, m = plan[t]
+        chunks, back = plan[t]
         lp = landpos(r, t)
         land, so, z = "land%d" % t, "so%d" % t, CMPW // 2
         chunks_of = [[k for k, c in enumerate(CH[t]) if c[3] == s] for s in range(N)]
@@ -406,56 +366,52 @@ def rank_program(g, core, T, topo):
             to = V("rho%d" % t, 5 * i, 5 * i + nc)
             tt(to, at, V("pland%d" % t, 5 * slot(r, s) + o, 5 * slot(r, s) + o + nc), Alu.add)
             at = to
-        for b in range(4):
-            for a in range(4):
-                src = V("rho%d" % t, 10, 10 + nc, 1, 32 * a, 32 * a + 32)
-                to = V("msp", 32 * a, 128 * nc, 128, 32 * b, 32 * b + 32)
-                if a % 2:
-                    act(to, src, Act.Sign, bias=K - 0.5, scale=-1.0)
-                else:
-                    ts(to, src, float(K), 2.0, Alu.is_lt, Alu.mult)
+        mq, g0, lo1 = "mq%d" % t, CH[t][chunks[0]][0], WIN[t + 1][r][0]
+        even = [k for k in chunks if CH[t][k][0] - g0 == 128 * (k - chunks[0])]
+        for a in range(4):
+            ts(V(mq, 3 + a, 3 + 4 * len(even), 4, 0, 32), V("rho%d" % t, 10, 10 + len(even), 1, 32 * a, 32 * a + 32), float(K), None, Alu.is_lt)
+        for k in chunks[len(even):]:
+            c, i = CH[t][k], 10 + k - chunks[0]
+            for a in range(c[1], c[2]):
+                x = 3 + (c[0] - g0) // 32 + a
+                ts(V(mq, x, x + 1, 1, 0, 32), V("rho%d" % t, i, i + 1, 1, 32 * a, 32 * a + 32), float(K), None, Alu.is_lt)
         hook2()
+        start = 0.0
+        if back:
+            start, x = V("tot%d" % t, 0, 1, 1, 0, 32), V(mq, 3, 3 + 4 * nc, 1, 0, 32)
+            op("v", lambda: g.vector.tensor_reduce(start[0], x[0], AxisListType.X, Alu.add, negate=True), [x], [start])
+        nq = (NW[t + 1] + 16 * M - 1) // (16 * M)
+        for a in range(nq):
+            y = 3 + (lo1 + 16 * M * a - K - g0) // 32 + 5
+            n = y - min(2, y - 6)
+            scan(V("msp", B0 - 32 * (n - 6), B0 + FW, 32, 32 * a, 32 * a + 32), V("cz", 29 - n, 29, 1, 0, 32), V(mq, y - n, y, 1, 0, 32), start, Alu.mult, Alu.add)
         fillin(jobs)
-        pieces = runs([CH[t][k] for k in chunks], first, n)
-        x0, x1 = pieces[0][0], pieces[-1][0] + pieces[-1][2]
-        scan(V("mrep", x0, x1), V("carb", x0, x1), V("msp", x0, x1), 0.0, Alu.mult, Alu.add)
+        scan(V("mrep"), V("carb"), V("msp", B0), 0.0, Alu.mult, Alu.add)
         fillin(jobs)
-        for x, y, w in pieces:
-            turn(V("mrow%d" % t, y, y + w), V("mrep", x, x + w))
+        turn(V("mrow%d" % t), V("mrep"))
         fillin(jobs)
         fb = "fb%d" % t
-        scan(V(fb, PAD + 1, PAD + n + 1), V("mrow%d" % t, 0, n), V("inc%d" % t, 0, n), float(2 * (first - mid)), Alu.add, Alu.add)
+        scan(V(fb), V("mrow%d" % t), V("inc"), 0.0 if back else -float(K), Alu.add, Alu.add)
         fillin(jobs)
-        jj, o = "jt%d" % t, 6
-        if back:
-            jj, o = "jj%d" % t, 0
-            ts(V(jj), V("jt%d" % t, 6, 18), V(fb, PAD + n, PAD + n + 1), None, Alu.add)
-            if t == 0:
-                ts(V("xc%d" % t), V(jj, 6, 7), float(SW), None, Alu.mult)
-            else:
-                act(V("xc%d" % t), V(jj, 6, 7), Act.Copy, scale=float(SW))
-        nv = min(m, NV[t])
-        hm = m - nv
-        for i in range(m):
-            x, y = slice_of(t, i)
-            ts(V("ch%d" % t, CW * i, CW * i + SW), V(fb, x, y), V(jj, o + i, o + i + 1), V(jj, o + 6 + i, o + 7 + i), Alu.max, Alu.min)
-            if i < hm:
-                act(V("fs%d" % t, CW * i, CW * i + CW), V("ch%d" % t, CW * i, CW * i + CW), Act.Copy, accum=V("sm%d" % t, i, i + 1))
-        cu, h = "cu%d" % t, CW // 2
-        scan(V(cu, 1, 1 + nv * h), V("ch%d" % t, hm * CW, m * CW, 2), V("ch%d" % t, hm * CW + 1, m * CW, 2), 0.0, Alu.add, Alu.add)
+        for i in range(M):
+            ts(V("ch", CW * i, CW * i + SW), V(fb, 31 + 16 * i, 31 + 16 * i + SW), V("jt", M + i, M + i + 1), V("jt", 2 * M + i, 2 * M + i + 1), Alu.max, Alu.min)
+        h = CW // 2
+        scan(V("cu", 1), V("ch", 0, M * CW, 2), V("ch", 1, M * CW, 2), 0.0, Alu.add, Alu.add)
         fillin(jobs)
-        sm, W = V("sm%d" % t, 0, m), NW[t]
-        tt(V("sm%d" % t, hm, m), V(cu, h, nv * h + 1, h), V(cu, 0, (nv - 1) * h + 1, h), Alu.subtract)
-        ts(V("qi%d" % t, 0, m), sm, V("xc%d" % t), -1.0 / 6, Alu.subtract, Alu.mult)
-        ts(V("ws%d" % t, 0, m), sm, V("xc%d" % t), -0.5 * W, Alu.subtract, Alu.mult)
-        ts(V("wy%d" % t, 0, m), V("qi%d" % t, 0, m), float(1 - 3 * W), float(W), Alu.mult, Alu.add)
-        tt(V("ll%d" % t, 0, m), V("ws%d" % t, 0, m), V("wy%d" % t, 0, m), Alu.add)
-        for b in range(4):
-            for a in range(4):
-                copy("s" if (a + b) % 2 and (a, b) != (0, 1) else "v", V("wf%d" % t, a, 4 * m, 4, 32 * b, 32 * b + 32), V("ll%d" % t, 0, m, 1, 32 * a, 32 * a + 32))
+        sm, W = V("sm%d" % t), NW[t]
+        tt(sm, V("cu", h, M * h + 1, h), V("cu", 0, (M - 1) * h + 1, h), Alu.subtract)
+        fillin(jobs)
+        ts(V("qi%d" % t), sm, V("xc%d" % t), -1.0 / 3, Alu.subtract, Alu.mult)
+        ts(V("ws%d" % t), sm, V("xc%d" % t), -float(W), Alu.subtract, Alu.mult)
+        ts(V("wy%d" % t), V("qi%d" % t), float(1 - 3 * W), float(W), Alu.mult, Alu.add)
+        fillin(jobs)
+        n = NW[t + 1] // 16
+        for a in range(nq):
+            tt(V("wf%d" % t, M * a, M * a + M, 1, 0, 32), V("ws%d" % t, 0, M, 1, 32 * a, 32 * a + 32), V("wy%d" % t, 0, M, 1, 32 * a, 32 * a + 32), Alu.add)
         while jobs:
             fillin(jobs)
-        copy("v", V("wu%d" % t, 0, 4 * m), V("wf%d" % t, 0, 4 * m))
+        for b in range(4):
+            copy("v", V("wu%d" % t, 0, n, 1, 32 * b, 32 * b + 32), V("wf%d" % t, 0, n, 1, 0, 32))
 
     def pick(t, x=0, y=None):
         y, w = y or NW[t + 1], 3 * NW[t]
@@ -480,7 +436,6 @@ def rank_program(g, core, T, topo):
     inner = jobs.pop(0)
 
     def flight_of_scores0():
-        last_steps(0)
         quant("a", 0, 512, V("at"))
 
     def flight_of_counts0():
@@ -488,7 +443,6 @@ def rank_program(g, core, T, topo):
         quant("b", 0, 512, V("bt"))
         kidq(0, [inner])[0]()
         kids(0, "ssssssss", range(4, 5), own0)
-        steps(1)
         for i in range(3):
             op("g", lambda: g.iota(T.tn0[:, NW[0] * i:NW[0] * i + NW[0]], [[4, NW[0]]], 4 * WIN[0][r][0] + (2 if i == 2 else 0), 0, allow_small_or_imprecise_dtypes=True),
                [], [V("tn0", NW[0] * i, NW[0] * i + NW[0])])
@@ -505,12 +459,11 @@ def rank_program(g, core, T, topo):
     bank[0] = 0
 
     def flight_of_scores1():
-        last_steps(1)
-        kids(1, "sss", range(3))
+        kids(1, "ss", range(2))
         quant("w", 0, 128, V("wt"))
 
     def flight_of_counts1():
-        kids(1, "ssssvsvs", range(3, 8))
+        kids(1, "ssssvsvs", range(2, 8))
         for job in kidq(1, [(0, 0, NW[1]), (1, 0, NW[1])]):
             job()
 

@@ -9,17 +9,19 @@ NEED = ([(0, 288), (0, 576), (448, 1024), (736, 1024)], [(0, 288), (0, 576), (51
 F32, BF, I32, U16 = "float32", "bfloat16", "int32", "uint16"
 M = 6
 SW = 81
-CW = 82
+CW = 84
 FW = 192
 B0 = 512
 CMPW = 448
 
 SCRATCH = {
-    "xt": ("sbuf", [128, 1024], BF), "uin": ("sbuf", [128, 8], BF), "ut": ("sbuf", [128, 512], BF), "uz": ("sbuf", [128, 128], BF),
+    "xt": ("sbuf", [128, 1024], BF), "uin": ("sbuf", [128, 8], BF), "ut": ("sbuf", [128, 512], BF),
+    "uz": ("sbuf", [128, 192], BF), "one": ("sbuf", [128, 128], BF), "nid": ("sbuf", [128, 128], BF),
     "at": ("sbuf", [128, 2048], BF), "bt": ("sbuf", [128, 2048], BF), "wt": ("sbuf", [128, 512], BF),
     "msp": ("sbuf", [128, B0 + FW], BF), "mrep": ("sbuf", [128, FW], BF), "carb": ("sbuf", [128, FW], BF), "inc": ("sbuf", [128, FW], BF),
-    "cz": ("sbuf", [128, 32], BF), "jt": ("sbuf", [128, 18], F32), "ch": ("sbuf", [128, M * CW], BF), "cu": ("sbuf", [128, 1 + M * CW // 2], F32),
-    "pi": ("sbuf", [128, 4], I32), "dcol": ("sbuf", [128, 3], F32),
+    "cz": ("sbuf", [128, 32], BF), "jt": ("sbuf", [128, 18], F32), "ch": ("sbuf", [128, M * CW], BF),
+    "cu": ("sbuf", [128, M * CW], BF), "car2": ("sbuf", [128, M * CW], BF),
+    "pi": ("sbuf", [128, 4], I32), "dcol": ("sbuf", [128, 4], F32),
     "psc": ("psum", [128, 2048], F32), "pch": ("psum", [128, 2048], F32),
     "ysb": ("sbuf", [128, 288], F32), "hsr": ("sbuf", [128, 288], F32),
     "tn0": ("sbuf", [128, 1248], F32), "tn1": ("sbuf", [128, 1056], F32),
@@ -29,9 +31,9 @@ for _q, _n in (("u", 128), ("a", 512), ("b", 512), ("w", 128), ("r0", 1248), ("r
     SCRATCH[_q + "s"] = ("sbuf", [128, _n], "uint8")
 for _t in range(2):
     for _n, _w, _d in (("ha", 1664, BF), ("hb", 1664, BF), ("own", 4, F32), ("land", 8, F32), ("cmp", 9 * CMPW, BF),
-                       ("eq", 384, BF), ("sg", 3 * 320, BF), ("sj", 3 * 320, BF), ("so", 9 * CMPW // 2, BF), ("acc", 3, F32),
-                       ("pland", 16, BF), ("rho", 15, F32), ("mrow", FW, BF), ("fb", FW, BF), ("mq", 32, BF), ("tot", 1, F32), ("xc", 1, F32),
-                       ("sm", 6, F32), ("qi", 6, I32), ("ws", 6, F32), ("wy", 6, F32), ("wf", 24, F32), ("wu", 24, U16)):
+                       ("eq", 384, BF), ("tie", 384, BF), ("sg", 3 * 320, BF), ("sj", 3 * 320, BF), ("so", 9 * CMPW // 2, BF), ("acc", 3, F32),
+                       ("pland", 16, BF), ("rho", 15, BF), ("mrow", FW, BF), ("fb", FW, BF), ("mq", 32, BF), ("tot", 1, F32), ("xc", 1, F32),
+                       ("qi", 6, I32), ("ws", 6, F32), ("wy", 6, F32), ("wf", 24, F32), ("wu", 24, U16)):
         SCRATCH["%s%d" % (_n, _t)] = ("sbuf", [128, _w], _d)
 SEMAPHORES = ["v", "s", "p", "gc", "sent", "arrw", "dx0", "dx1", "du", "da", "db", "dw", "out"] + ["%s%d_%d" % (k, t, r) for k in ("arr", "cnt") for t in range(2) for r in range(N)]
 
@@ -55,7 +57,7 @@ def rank_program(g, core, T, topo):
             return x[2] // 512 <= (y[3] - 1) // 512 and y[2] // 512 <= (x[3] - 1) // 512
         if x[6] <= y[5] or y[6] <= x[5] or x[3] <= y[2] or y[3] <= x[2]:
             return False
-        return not (x[4] == y[4] and x[4] > 1 and (x[2] - y[2]) % x[4] != 0)
+        return not set(range(x[2], x[3], x[4])).isdisjoint(range(y[2], y[3], y[4]))
 
     def need(q, reads, writes):
         todo = {}
@@ -215,26 +217,35 @@ def rank_program(g, core, T, topo):
     op("g", lambda: g.iota(T.jt[:, 0:M], [[16, M]], -1, 0, allow_small_or_imprecise_dtypes=True), [], [V("jt", 0, M)])
     op("v", lambda: g.vector.tensor_scalar(T.pi[:, 1:2], T.pi[:, 0:1], 96, None, Alu.bitwise_and), [V("pi", 0, 1)], [V("pi", 1, 2)])
     op("v", lambda: g.vector.tensor_scalar(T.pi[:, 2:3], T.pi[:, 0:1], 15, None, Alu.bitwise_and), [V("pi", 0, 1)], [V("pi", 2, 3)])
-    fill(V("msp", B0), 0.0)
-    fill(V("carb"), 1.0)
-    fill(V("inc"), 1.0)
-    fill(V("cz"), 1.0)
-    fill(V("cu", 0, 1), 0.0)
-    for t in range(2):
-        fill(V("mq%d" % t), 0.0)
     ts(V("dcol", 0, 1), V("pi", 2, 3), 1.0, None, Alu.mult)
-    ts(V("dcol", 1, 2), V("pi", 1, 2), 3.0 * 16 * M / 32, None, Alu.mult)
-    fill(V("carb", 0, FW, 32), 0.0)
-    fill(V("inc", 0, 32), 0.0)
-    fill(V("cz", 24, 32), 0.0)
-    act(V("jt", M, 2 * M), V("jt", 0, M), Act.Identity, bias=V("dcol", 0, 1))
-    act(V("jt", 2 * M, 3 * M), V("jt", M, 2 * M), Act.Identity, bias=3.0)
-    act(V("ch", SW, M * CW, CW), V("jt", 0, M), Act.Identity, bias=-3.0 - SW, scale=-3.0 - SW)
-    act(V("dcol", 2, 3), V("dcol", 0, 1), Act.Identity, bias=V("dcol", 1, 2), scale=float(SW))
+    ts(V("dcol", 1, 2), V("pi", 1, 2), 16.0 * M / 32, None, Alu.mult)
+    fill(V("one"), 1.0)
+    fill(V("car2"), 1.0)
+    fill(V("car2", 0, M * CW, CW), 0.0)
+    op("g", lambda: g.affine_select(T.nid[:], T.one[:], [[-1, 128]], Alu.not_equal, 0.0, 0, 1), [V("one")], [V("nid")])
+
+    def put(out, c):
+        act(out, V("uz", 0, len(range(out[2], out[3], out[4]))), Act.Identity, bias=c)
+    put(V("msp", B0), 0.0)
+    put(V("carb"), 1.0)
+    put(V("inc", 32), 1.0)
+    put(V("inc", 0, 32), 0.0)
+    put(V("cz", 0, 24), 1.0)
+    put(V("cz", 24, 32), 0.0)
     for t in range(2):
-        act(V("xc%d" % t), V("dcol", 2, 3), Act.Identity, bias=float(3 * (WIN[t + 1][r][0] - K - WIN[t][r][0]) + 2 * SW - 3))
+        put(V("mq%d" % t), 0.0)
+    put(V("carb", 0, FW, 32), 0.0)
+    act(V("jt", M, 2 * M), V("jt", 0, M), Act.Identity, bias=V("dcol", 0, 1))
+    act(V("ch", SW, M * CW, CW), V("jt", 0, M), Act.Identity, bias=-3.0 - SW, scale=-3.0 - SW)
+    act(V("dcol", 2, 3), V("dcol", 0, 1), Act.Identity, bias=64.0, scale=-64.0)
+    act(V("dcol", 3, 4), V("dcol", 0, 1), Act.Identity, bias=SW - 64.0, scale=64.0 - SW)
+    act(V("jt", 2 * M, 3 * M), V("jt", M, 2 * M), Act.Identity, bias=3.0)
+    for i in range(2):
+        put(V("ch", SW + 1 + i, M * CW, CW), V("dcol", 2 + i, 3 + i))
+    for t in range(2):
+        act(V("xc%d" % t), V("dcol", 1, 2), Act.Identity, bias=float(WIN[t + 1][r][0] - K - WIN[t][r][0] + 80 + NW[t]))
     for k in range(4):
-        ts(V("ut", k, 512, 4), V("uz"), V("uin", k, k + 1), None, Alu.add)
+        ts(V("ut", k, 512, 4), V("uz", 0, 128), V("uin", k, k + 1), None, Alu.add)
     quant("u", 0, 128, V("ut"))
 
     def border_to(s, plane):
@@ -316,34 +327,35 @@ def rank_program(g, core, T, topo):
         def row(a, b):
             return V("psc", a - lo, b - lo)
 
-        def total_of(k, w):
+        def total_of(k, w, start=0.0):
             x, y = CMPW * k, w // 2
-            scan(V(so, 9 * (z - y) + k, 9 * (z - 1) + k + 1, 9), V("cmp%d" % t, x, x + y), V("cmp%d" % t, x + y, x + w), 0.0, Alu.add, Alu.add)
+            scan(V(so, 9 * (z - y) + k, 9 * (z - 1) + k + 1, 9), V("cmp%d" % t, x, x + y), V("cmp%d" % t, x + y, x + w), start, Alu.add, Alu.add)
 
         def part(k, m=1):
             return V(so, 9 * (z - 1) + k, 9 * (z - 1) + k + m, 9 if m == 1 else 1)
 
-        wide = {}
         for i, k in enumerate(mine):
             s = CH[t][k][0]
-            e = min(s + 128, hi)
+            e = s + 128
             val = V("own%d" % t, i, i + 1)
             x = CMPW * k
-            q = V("eq%d" % t, 128 * i, 128 * i + e - s)
-            d = V("cmp%d" % t, x + W, x + W + e - s)
+            q = V("eq%d" % t, 128 * i, 128 * i + 128)
             ts(q, row(s, e), val, None, Alu.is_equal)
-            op("g", lambda: g.affine_select(d[0], q[0], [[-1, e - s]], Alu.is_gt, 0.0, 0, 1), [q], [d])
-            if s > lo:
-                ts(V("cmp%d" % t, x, x + s - lo), row(lo, s), val, None, Alu.is_ge)
-            ts(V("cmp%d" % t, x + s - lo, x + W), row(s, hi), val, None, Alu.is_gt)
-            wide[k] = W + e - s
+            ts(V("cmp%d" % t, x, x + e - lo), row(lo, e), val, None, Alu.is_ge)
+            scan(V("tie%d" % t, 128 * i, 128 * i + 128), V("nid"), q, 0.0, Alu.mult, Alu.subtract)
+            if e < hi:
+                ts(V("cmp%d" % t, x + e - lo, x + W), row(e, hi), val, None, Alu.is_gt)
+        for i, k in enumerate(mine):
+            total_of(k, W, V("tie%d" % t, 128 * i + 127, 128 * i + 128))
         flight1()
         first_r, second_r, third_r = sorted(others_r, key=lambda s: targets(T.cores[s]).index(core))
         byS, byV = (third_r, second_r) if len(chunks_of[second_r]) > len(chunks_of[third_r]) else (second_r, third_r)
         for i, k in enumerate(chunks_of[byS]):
             act(V("sg%d" % t, 320 * i, 320 * i + W), V("pch", 1536, 1536 + W), Act.Sign, bias=V(land, lp[k], lp[k] + 1), scale=-1.0)
+        for i, k in enumerate(chunks_of[byS]):
             act(V("sj%d" % t, 320 * i, 320 * i + W), V("sg%d" % t, 320 * i, 320 * i + W), Act.Relu, scale=1.0 if r < byS else -1.0, accum=V("acc%d" % t, i, i + 1))
-            act(part(k), V("acc%d" % t, i, i + 1), Act.Copy, scale=-1.0 if r < byS else 1.0, bias=float(W) if r < byS else 0.0)
+        n = len(chunks_of[byS])
+        act(part(chunks_of[byS][0], n), V("acc%d" % t, 0, n), Act.Copy, scale=-1.0 if r < byS else 1.0, bias=float(W) if r < byS else 0.0)
         last = None
         for s in (first_r, byV):
             for k in chunks_of[s]:
@@ -352,29 +364,32 @@ def rank_program(g, core, T, topo):
                     total_of(last, W)
                 last = k
         total_of(last, W)
-        for k in mine:
-            total_of(k, wide[k])
         for h in sorted(half, key=lambda h: core not in h):
             cs = [c for c in others if c in h]
             k0 = group(T.rank_of(h[0]), t)[0]
             send([T["pland%d" % t][:, 5 * slot(T.rank_of(c), r):5 * slot(T.rank_of(c), r) + 5] for c in cs], part(k0, 5), cs, "cnt%d_%d" % (t, r))
-        flight2()
         k0, nc = chunks[0], len(chunks)
+        flight2()
+        at = V("rho%d" % t, 0, nc)
+        ts(at, part(k0, nc), -1.0, float(K), Alu.mult, Alu.add)
         o = chunks[0] - group(r, t)[0]
-        at = part(k0, nc)
-        for i, s in enumerate(sorted(others_r, key=lambda s: (s // 2 != r // 2, near(core, T.cores[s])))):
-            to = V("rho%d" % t, 5 * i, 5 * i + nc)
-            tt(to, at, V("pland%d" % t, 5 * slot(r, s) + o, 5 * slot(r, s) + o + nc), Alu.add)
+        srt = sorted(others_r, key=lambda s: (s // 2 != r // 2, near(core, T.cores[s])))
+        for i, s in enumerate(srt[:2]):
+            to = V("rho%d" % t, 5 * i + 5, 5 * i + 5 + nc)
+            tt(to, at, V("pland%d" % t, 5 * slot(r, s) + o, 5 * slot(r, s) + o + nc), Alu.subtract)
             at = to
-        mq, g0, lo1 = "mq%d" % t, CH[t][chunks[0]][0], WIN[t + 1][r][0]
+        mq, g0, lo1, l0 = "mq%d" % t, CH[t][chunks[0]][0], WIN[t + 1][r][0], 5 * slot(r, srt[2]) + o
         even = [k for k in chunks if CH[t][k][0] - g0 == 128 * (k - chunks[0])]
+
+        def mask(to, i, n, a):
+            tt(to, V("pland%d" % t, l0 + i, l0 + i + n, 1, 32 * a, 32 * a + 32), V("rho%d" % t, 10 + i, 10 + i + n, 1, 32 * a, 32 * a + 32), Alu.is_lt)
         for a in range(4):
-            ts(V(mq, 3 + a, 3 + 4 * len(even), 4, 0, 32), V("rho%d" % t, 10, 10 + len(even), 1, 32 * a, 32 * a + 32), float(K), None, Alu.is_lt)
+            mask(V(mq, 3 + a, 3 + 4 * len(even), 4, 0, 32), 0, len(even), a)
         for k in chunks[len(even):]:
-            c, i = CH[t][k], 10 + k - chunks[0]
+            c = CH[t][k]
             for a in range(c[1], c[2]):
                 x = 3 + (c[0] - g0) // 32 + a
-                ts(V(mq, x, x + 1, 1, 0, 32), V("rho%d" % t, i, i + 1, 1, 32 * a, 32 * a + 32), float(K), None, Alu.is_lt)
+                mask(V(mq, x, x + 1, 1, 0, 32), k - chunks[0], 1, a)
         hook2()
         start = 0.0
         if back:
@@ -395,15 +410,13 @@ def rank_program(g, core, T, topo):
         fillin(jobs)
         for i in range(M):
             ts(V("ch", CW * i, CW * i + SW), V(fb, 31 + 16 * i, 31 + 16 * i + SW), V("jt", M + i, M + i + 1), V("jt", 2 * M + i, 2 * M + i + 1), Alu.max, Alu.min)
-        h = CW // 2
-        scan(V("cu", 1), V("ch", 0, M * CW, 2), V("ch", 1, M * CW, 2), 0.0, Alu.add, Alu.add)
+        scan(V("cu"), V("car2"), V("ch"), 0.0, Alu.mult, Alu.add)
         fillin(jobs)
-        sm, W = V("sm%d" % t), NW[t]
-        tt(sm, V("cu", h, M * h + 1, h), V("cu", 0, (M - 1) * h + 1, h), Alu.subtract)
         fillin(jobs)
-        ts(V("qi%d" % t), sm, V("xc%d" % t), -1.0 / 3, Alu.subtract, Alu.mult)
-        ts(V("ws%d" % t), sm, V("xc%d" % t), -float(W), Alu.subtract, Alu.mult)
-        ts(V("wy%d" % t), V("qi%d" % t), float(1 - 3 * W), float(W), Alu.mult, Alu.add)
+        sm, W = V("cu", CW - 1, M * CW, CW), NW[t]
+        ts(V("qi%d" % t), sm, -1.0 / 3, None, Alu.mult)
+        ts(V("ws%d" % t), sm, -float(W), V("xc%d" % t), Alu.mult, Alu.add)
+        ts(V("wy%d" % t), V("qi%d" % t), float(1 - 3 * W), None, Alu.mult)
         fillin(jobs)
         n = NW[t + 1] // 16
         for a in range(nq):
@@ -454,8 +467,14 @@ def rank_program(g, core, T, topo):
         for x in border:
             kids(0, "ssssssss", range(4), x)
     order(0, flight_of_scores0, flight_of_counts0, rest_kids, kidq(0, jobs))
-    pick(0)
+    mine1 = [c for c in CH[1] if c[3] == r]
+    o0, o1 = mine1[0][0] - WIN[1][r][0], mine1[-1][0] + 128 - WIN[1][r][0]
+    pick(0, o0, o0 + 128)
+    pick(0, o0 + 128, o1)
     score(1)
+    for x, y in ((0, o0), (o1, NW[1])):
+        if y > x:
+            pick(0, x, y)
     bank[0] = 0
 
     def flight_of_scores1():
@@ -476,12 +495,11 @@ def rank_program(g, core, T, topo):
     for x, y in cut:
         pick(1, x, y)
     outs = [mm(("psc", i), "w", 0, "r2", x, y - x) for i, (x, y) in enumerate(cut)]
+    for k in range(4):
+        dma("s", T.osc[4 * k:4 * k + 4, :], T.r2s[32 * k:32 * k + 4, :], "out", [V("r2s")], [])
     numbers(1, V("hsr"))
-
     for x, y in cut:
         dma("y", T.oc[:, 4 * x:4 * y], codes("r2c", x, y), "out", [V("r2c", x, y)], [])
-    for k in range(4):
-        dma("y", T.osc[4 * k:4 * k + 4, :], T.r2s[32 * k:32 * k + 4, :], "out", [V("r2s")], [])
     dma("s", T.hs[:], T.hsr[0:1, :], "out", [V("hsr")], [])
     for o, (x, y) in zip(outs, cut):
         copy("v", V("ysb", x, y), o)

@@ -1,41 +1,44 @@
 from concourse.bass import DstId, RemoteDMATransfer
-from concourse.mybir import dt, AluOpType as Alu, AxisListType, ActivationFunctionType as Act
+from concourse.mybir import dt, AluOpType as Alu, ActivationFunctionType as Act
 
 N, P, K, E = 4, 256, 64, 288
-CH = ([(128 * c, 0, 4, c // 2) for c in range(8)],
-      [(0, 0, 4, 0), (128, 0, 4, 0), (256, 0, 4, 1), (384, 0, 4, 1), (448, 2, 4, 1), (576, 0, 4, 2), (704, 0, 4, 2), (832, 0, 4, 3), (960, 0, 4, 3)])
-WIN = ([(0, 288), (160, 576), (448, 864), (736, 1024)], [(0, 288), (224, 576), (512, 864), (800, 1088)], [(E * r, E * r + E) for r in range(N)])
-NEED = ([(0, 288), (0, 576), (448, 1024), (736, 1024)], [(0, 288), (0, 576), (512, 1088), (800, 1088)])
+OWNER = ([0, 0, 1, 1, 2, 2, 3, 3], [0, 0, 0, 1, 1, 2, 2, 3, 3])
+OFF = (0, -64)
+NEED = ([(0, 3), (0, 5), (3, 5), (5, 3)], [(0, 3), (0, 5), (4, 5), (6, 3)])
+WIN = ([(0, 320), (160, 576), (448, 864), (736, 1024)], [(0, 320), (224, 576), (512, 864), (800, 1088)], [(E * r, E * r + E) for r in range(N)])
 F32, BF, I32, U16 = "float32", "bfloat16", "int32", "uint16"
 M = 6
+MV = 5
 SW = 81
 CW = 84
 FW = 192
 B0 = 512
 CMPW = 448
+BIG = 1.5 * 2 ** 23
 
 SCRATCH = {
-    "xt": ("sbuf", [128, 1024], BF), "uin": ("sbuf", [128, 8], BF), "ut": ("sbuf", [128, 512], BF),
-    "uz": ("sbuf", [128, 192], BF), "one": ("sbuf", [128, 128], BF), "nid": ("sbuf", [128, 128], BF),
+    "xt": ("sbuf", [128, 1024], BF), "u0": ("sbuf", [128, 512], BF), "ut": ("sbuf", [128, 512], BF),
+    "uz": ("sbuf", [128, 192], BF), "one": ("sbuf", [128, 136], BF), "nid": ("sbuf", [128, 136], BF),
     "at": ("sbuf", [128, 2048], BF), "bt": ("sbuf", [128, 2048], BF), "wt": ("sbuf", [128, 512], BF),
     "msp": ("sbuf", [128, B0 + FW], BF), "mrep": ("sbuf", [128, FW], BF), "carb": ("sbuf", [128, FW], BF), "inc": ("sbuf", [128, FW], BF),
-    "cz": ("sbuf", [128, 32], BF), "jt": ("sbuf", [128, 18], F32), "ch": ("sbuf", [128, M * CW], BF),
-    "cu": ("sbuf", [128, M * CW], BF), "car2": ("sbuf", [128, M * CW], BF),
+    "cz": ("sbuf", [128, 32], BF), "jt": ("sbuf", [128, 2 * M], F32), "jb": ("sbuf", [128, 2 * M + 2], F32), "ch": ("sbuf", [128, M * CW], BF),
+    "cu": ("sbuf", [128, M * CW], BF), "car2": ("sbuf", [128, MV * CW], BF),
     "pi": ("sbuf", [128, 4], I32), "dcol": ("sbuf", [128, 4], F32),
     "psc": ("psum", [128, 2048], F32), "pch": ("psum", [128, 2048], F32),
+    "tri": ("sbuf", [128, 8 * M], F32), "trd": ("sbuf", [128, 8 * M], F32), "tif": ("sbuf", [128, 132], F32),
     "ysb": ("sbuf", [128, 288], F32), "hsr": ("sbuf", [128, 288], F32),
     "tn0": ("sbuf", [128, 1248], F32), "tn1": ("sbuf", [128, 1056], F32),
 }
-for _q, _n in (("u", 128), ("a", 512), ("b", 512), ("w", 128), ("r0", 1248), ("r1", 1056), ("r2", 288)):
+for _q, _n in (("z", 128), ("u", 128), ("a", 512), ("b", 512), ("w", 128), ("r0", 1248), ("r1", 1056), ("r2", 288)):
     SCRATCH[_q + "c"] = ("sbuf", [128, _n], "float8_e4m3fn_x4")
     SCRATCH[_q + "s"] = ("sbuf", [128, _n], "uint8")
 for _t in range(2):
     for _n, _w, _d in (("ha", 1664, BF), ("hb", 1664, BF), ("own", 4, F32), ("land", 8, F32), ("cmp", 9 * CMPW, BF),
-                       ("eq", 384, BF), ("tie", 384, BF), ("sg", 3 * 320, BF), ("sj", 3 * 320, BF), ("so", 9 * CMPW // 2, BF), ("acc", 3, F32),
-                       ("pland", 16, BF), ("rho", 15, BF), ("mrow", FW, BF), ("fb", FW, BF), ("mq", 32, BF), ("tot", 1, F32), ("xc", 1, F32),
-                       ("qi", 6, I32), ("ws", 6, F32), ("wy", 6, F32), ("wf", 24, F32), ("wu", 24, U16)):
+                       ("eq", 392, BF), ("tie", 256, BF), ("sg", 3 * 320, BF), ("sj", 3 * 320, BF), ("so", 9 * CMPW // 2, BF), ("acc", 3, F32),
+                       ("pland", 24, BF), ("rho", 24, BF), ("mrow", FW, BF), ("fb", FW, BF), ("mq", 32, BF), ("xc", 1, F32),
+                       ("ac2", 2, F32), ("sj2", 192, BF), ("wf", 16 * M, F32), ("wu", 24, U16)):
         SCRATCH["%s%d" % (_n, _t)] = ("sbuf", [128, _w], _d)
-SEMAPHORES = ["v", "s", "p", "gc", "sent", "arrw", "dx0", "dx1", "du", "da", "db", "dw", "out"] + ["%s%d_%d" % (k, t, r) for k in ("arr", "cnt") for t in range(2) for r in range(N)]
+SEMAPHORES = ["v", "s", "p", "gc", "sent", "arrl", "arrr", "dx0", "dx1", "du", "da", "db", "dw", "out"] + ["%s%d_%d" % (k, t, r) for k in ("arr", "cnt") for t in range(2) for r in range(N)]
 
 
 def rank_program(g, core, T, topo):
@@ -51,6 +54,10 @@ def rank_program(g, core, T, topo):
             c1 = SCRATCH[name][1][1]
         ap = T[name][p0:p1, c0:c1] if step == 1 else T[name][p0:p1, c0:c1:step]
         return (ap, name, c0, c1, step, p0, p1)
+
+    def back(name, c0, c1, step=1, p0=0, p1=128):
+        last = c0 + (c1 - 1 - c0) // step * step
+        return (T[name][p0:p1, last:(c0 - 1 if c0 else None):-step], name, c0, c1, step, p0, p1)
 
     def clash(x, y):
         if SCRATCH[x[1]][0] == "psum":
@@ -130,6 +137,10 @@ def rank_program(g, core, T, topo):
     def fill(out, c):
         op("v", lambda: g.vector.memset(out[0], c), [], [out])
 
+    def count(out, step, base):
+        n = len(range(out[2], out[3], out[4]))
+        op("g", lambda: g.iota(out[0], [[step, n]], base, 0, allow_small_or_imprecise_dtypes=True), [], [out])
+
     def quant(q, a, b, in_):
         c, s = V(q + "c", a, b), V(q + "s", a, b)
         op("v", lambda: g.vector.quantize_mx(c[0], s[0], in_[0]), [in_], [c, s])
@@ -172,81 +183,86 @@ def rank_program(g, core, T, topo):
     NW = [WIN[t][r][1] - WIN[t][r][0] for t in range(3)]
     C = (NW[0], NW[1], 0)
     others = targets(core)
-    others_r = [T.rank_of(c) for c in others]
+    senders = sorted([T.rank_of(c) for c in others], key=lambda s: targets(T.cores[s]).index(core))
     ENG = len(engines(others))
-    half = (T.cores[:N // 2], T.cores[N // 2:])
+    sig = 1.0 if r < N // 2 else -1.0
 
     def slot(me, s):
-        return s if s < me else s - 1
+        return 8 * (s if s < me else s - 1)
 
-    def group(me, t):
-        return list(range(5)) if me < N // 2 else list(range(len(CH[t]) - 5, len(CH[t])))
+    def take(t, me):
+        return 0 if me < N // 2 else len(OWNER[t]) - 5
+
+    def counted(s):
+        cs = targets(T.cores[s])
+        return [[c for c in cs if (T.rank_of(c) // 2 == s // 2) == same] for same in (True, False)]
 
     def landpos(me, t):
-        return {k: i for i, k in enumerate([k for k, c in enumerate(CH[t]) if c[3] != me])}
+        return {k: i for i, k in enumerate([k for k, s in enumerate(OWNER[t]) if s != me])}
+
+    def chunks_of(t, s):
+        return [k for k, o in enumerate(OWNER[t]) if o == s]
 
     halves = (0, 1) if r else (1, 0)
     for i in halves:
         dma("y", T.xt[:, 512 * i:512 * i + 512], T.x[:, 512 * i:512 * i + 512], "dx%d" % i, [], [V("xt", 512 * i, 512 * i + 512)])
-    dma("s", T.uin[:, 0:4], T.u[:, 0:4], "du", [], [V("uin", 0, 4)])
+    dma("s", T.u0[:, 0:8], T.u[:, 0:8], "du", [], [V("u0", 0, 8)])
     dma("y", T.at[:], T.a[:], "da", [], [V("at")])
     dma("y", T.bt[:], T.b[:], "db", [], [V("bt")])
-    dma("y", T.wt[:], T.w[:], "dw", [], [V("wt")])
 
     own0 = (P * r - WIN[0][r][0], P * r - WIN[0][r][0] + P)
     nb = [s for s in (r - 1, r + 1) if 0 <= s < N]
-    wviews = []
-    for s in nb:
-        a, b = (0, own0[0]) if s < r else (own0[1], NW[0])
-        wviews += [V("r0c", C[0] + a, C[0] + b), V("r0s", C[0] + a, C[0] + b)]
-    arrive("arrw", 2 * ENG * len(nb), wviews)
+    left, right = [(0, own0[0])] * (r > 0), [(own0[1], NW[0])] * (r < N - 1)
+    for sem, side in (("arrl", left), ("arrr", right)):
+        for a, b in side:
+            arrive(sem, 2 * ENG, [V("r0c", C[0] + a, C[0] + b), V("r0s", C[0] + a, C[0] + b)])
     for t in range(2):
-        for s in others_r:
-            cols = [landpos(r, t)[k] for k, c in enumerate(CH[t]) if c[3] == s]
+        for s in senders:
+            cols = [landpos(r, t)[k] for k in chunks_of(t, s)]
             arrive("arr%d_%d" % (t, s), ENG, [V("land%d" % t, cols[0], cols[-1] + 1)])
-            arrive("cnt%d_%d" % (t, s), ENG, [V("pland%d" % t, 5 * slot(r, s), 5 * slot(r, s) + 5)])
-
-    plan = []
-    for t in range(2):
-        a, b = NEED[t][r]
-        chunks = [k for k, c in enumerate(CH[t]) if c[0] + 32 * c[2] > a and c[0] + 32 * c[1] < b]
-        plan.append((chunks, a > 0))
+            arrive("cnt%d_%d" % (t, s), ENG, [V("pland%d" % t, slot(r, s), slot(r, s) + 5)])
+    x = landpos(r, 0)[chunks_of(0, senders[0])[0]]
+    dma("y", T.wt[:], T.w[:], "dw", [V("land0", x, x + 1)], [V("wt")])
 
     fill(V("uz"), 0.0)
+    fill(V("u0", 8), 0.0)
     op("g", lambda: g.iota(T.pi[:, 0:1], [[0, 1]], 0, 1), [], [V("pi", 0, 1)])
-    op("g", lambda: g.iota(T.jt[:, 0:M], [[16, M]], -1, 0, allow_small_or_imprecise_dtypes=True), [], [V("jt", 0, M)])
+    count(V("jt", 0, M), 16, -1)
     op("v", lambda: g.vector.tensor_scalar(T.pi[:, 1:2], T.pi[:, 0:1], 96, None, Alu.bitwise_and), [V("pi", 0, 1)], [V("pi", 1, 2)])
     op("v", lambda: g.vector.tensor_scalar(T.pi[:, 2:3], T.pi[:, 0:1], 15, None, Alu.bitwise_and), [V("pi", 0, 1)], [V("pi", 2, 3)])
+    fill(V("one"), 1.0)
     ts(V("dcol", 0, 1), V("pi", 2, 3), 1.0, None, Alu.mult)
     ts(V("dcol", 1, 2), V("pi", 1, 2), 16.0 * M / 32, None, Alu.mult)
-    fill(V("one"), 1.0)
+    op("g", lambda: g.affine_select(T.nid[:], T.one[:], [[-1, 136]], Alu.not_equal, 0.0, 0, 1), [V("one")], [V("nid")])
     fill(V("car2"), 1.0)
-    fill(V("car2", 0, M * CW, CW), 0.0)
-    op("g", lambda: g.affine_select(T.nid[:], T.one[:], [[-1, 128]], Alu.not_equal, 0.0, 0, 1), [V("one")], [V("nid")])
+    fill(V("inc", 0, 32), 0.0)
+    fill(V("car2", 0, MV * CW, CW), 0.0)
+    fill(V("cz", 0, 24), 1.0)
+    fill(V("cz", 24, 32), 0.0)
 
     def put(out, c):
         act(out, V("uz", 0, len(range(out[2], out[3], out[4]))), Act.Identity, bias=c)
-    put(V("msp", B0), 0.0)
+    m0 = B0 if sig > 0 else 0
+    put(V("msp", m0, m0 + FW), 0.0)
     put(V("carb"), 1.0)
     put(V("inc", 32), 1.0)
-    put(V("inc", 0, 32), 0.0)
-    put(V("cz", 0, 24), 1.0)
-    put(V("cz", 24, 32), 0.0)
     for t in range(2):
         put(V("mq%d" % t), 0.0)
+    for k in range(4):
+        put(V("ut", k, 512, 4), V("u0", k, k + 1))
     put(V("carb", 0, FW, 32), 0.0)
     act(V("jt", M, 2 * M), V("jt", 0, M), Act.Identity, bias=V("dcol", 0, 1))
-    act(V("ch", SW, M * CW, CW), V("jt", 0, M), Act.Identity, bias=-3.0 - SW, scale=-3.0 - SW)
-    act(V("dcol", 2, 3), V("dcol", 0, 1), Act.Identity, bias=64.0, scale=-64.0)
-    act(V("dcol", 3, 4), V("dcol", 0, 1), Act.Identity, bias=SW - 64.0, scale=64.0 - SW)
-    act(V("jt", 2 * M, 3 * M), V("jt", M, 2 * M), Act.Identity, bias=3.0)
+    act(V("ch", SW, M * CW, CW), V("jt", 0, M), Act.Identity, bias=sig * (-3.0 - SW), scale=sig * (-3.0 - SW))
+    act(V("jb", 0, M), V("jt", M, 2 * M), Act.Identity, scale=sig, bias=0.0 if sig > 0 else -3.0)
+    act(V("dcol", 2, 3), V("dcol", 0, 1), Act.Identity, bias=sig * 64.0, scale=sig * -64.0)
+    act(V("dcol", 3, 4), V("dcol", 0, 1), Act.Identity, bias=sig * (SW - 64.0), scale=sig * (64.0 - SW))
+    act(V("jb", M, 2 * M), V("jb", 0, M), Act.Identity, bias=3.0)
     for i in range(2):
         put(V("ch", SW + 1 + i, M * CW, CW), V("dcol", 2 + i, 3 + i))
+    act(V("jb", 2 * M, 2 * M + 2), V("jb", M - 1, 2 * M, M), Act.Identity, scale=-1.0)
     for t in range(2):
         act(V("xc%d" % t), V("dcol", 1, 2), Act.Identity, bias=float(WIN[t + 1][r][0] - K - WIN[t][r][0] + 80 + NW[t]))
-    for k in range(4):
-        ts(V("ut", k, 512, 4), V("uz", 0, 128), V("uin", k, k + 1), None, Alu.add)
-    quant("u", 0, 128, V("ut"))
+    short = len(chunks_of(1, r)) == 3
 
     def border_to(s, plane):
         sw = WIN[0][s]
@@ -254,74 +270,79 @@ def rank_program(g, core, T, topo):
         a, b = lo - WIN[0][r][0] + C[0], hi - WIN[0][r][0] + C[0]
         e = sw[1] - sw[0] - sw[0]
         c, d = lo + e, hi + e
+        sem = "arrl" if r < s else "arrr"
         if plane:
-            send([T.r0s[:, c:d]], V("r0s", a, b), [T.cores[s]], "arrw")
+            send([T.r0s[:, c:d]], V("r0s", a, b), [T.cores[s]], sem)
         else:
-            send([codes("r0c", c, d)], (codes("r0c", a, b),) + V("r0c", a, b)[1:], [T.cores[s]], "arrw")
+            send([codes("r0c", c, d)], (codes("r0c", a, b),) + V("r0c", a, b)[1:], [T.cores[s]], sem)
 
     for i in halves:
         quant("r0", C[0] + own0[0] + 128 * i, C[0] + own0[0] + 128 * i + 128, V("xt", 512 * i, 512 * i + 512))
         if i == halves[0]:
             border_to(nb[0], True)
+            quant("z", 0, 128, V("u0"))
 
     def score(t):
         q = "r%d" % t
         w0 = WIN[t][r][0] - C[t]
-        mine = [c for c in CH[t] if c[3] == r]
+        mine = chunks_of(t, r)
         n = len(mine)
-        for i, c in enumerate(mine):
-            mm(("psc", 1 + i), q, c[0] - w0, "u", 0, 128)
-        lo, hi = mine[0][0] + 32 * mine[0][1], mine[-1][0] + 32 * mine[-1][2]
-        mm(("psc", 0), "u", 0, q, lo - w0, hi - lo)
-        mm(("pch", 3), "u", 0, q, lo - w0, hi - lo)
+        for i in (range(n) if t else halves):
+            mm(("psc", 1 + i), q, 128 * mine[i] + OFF[t] - w0, "z", 0, 128)
         ow = V("own%d" % t, 0, n)
         copy("v", ow, V("psc", 512, 512 * n + 1, 512))
         outs = []
         for c in others:
-            p = landpos(T.rank_of(c), t)[CH[t].index(mine[0])]
+            p = landpos(T.rank_of(c), t)[mine[0]]
             outs.append(T["land%d" % t][:, p:p + n])
         send(outs, ow, others, "arr%d_%d" % (t, r))
+        if t == 0:
+            quant("u", 0, 128, V("ut"))
+        lo, hi = max(0, 128 * mine[0] + OFF[t]), 128 * mine[-1] + 128 + OFF[t]
+        mm(("psc", 0), "u", 0, q, lo - w0, hi - lo)
+        mm(("pch", 3), "u", 0, q, lo - w0, hi - lo)
 
     score(0)
     for s in nb:
         border_to(s, False)
         if s != nb[0]:
             border_to(s, True)
-    bank = [0]
+    count(V("tri", 1, 8 * M, 4), 0, -int(BIG))
+    count(V("tri", 3, 8 * M, 4), 0, 0)
+    count(V("trd", 0, 8 * M, 4), 0, 0)
+    count(V("trd", 1, 8 * M, 2), 0, 1)
+    for t in range(2):
+        count(V("trd", 4 * M * t + 2, 4 * M * t + 4 * M, 4), 0, 1 - 3 * NW[t])
+    count(V("tri", 4 * M - 1, 8 * M, 4 * M), 0, 16 * MV if sig > 0 else -1)
+    if short:
+        count(V("eq1", 384, 386), 0, -NW[1])
+    banks = {"s": [("pch", 0), ("pch", 1), ("pch", 2), ("psc", 1), ("psc", 2)], "v": [("psc", 3), ("psc", 0)]}
 
-    def kids(t, qs, part, cols=None):
+    def kid(t, i, e, cols=None):
         q, w = "r%d" % t, NW[t]
         lo, hi = cols or (0, w)
-        m0 = max(0, min(lo, hi - 128))
-        n = max(hi, m0 + 128) - m0
-        for i in part:
-            buf, k = (("pch", 0), ("pch", 1), ("pch", 2), ("psc", 1), ("psc", 2), ("psc", 3))[bank[0] % 6]
-            bank[0] += 1
-            mm((buf, k), "ab"[i // 4], 128 * (i % 4), q, C[t] + m0, n)
-            o = V(buf, 512 * k + lo - m0, 512 * k + hi - m0)
-            h = V("h%s%d" % ("ab"[i // 4], t), 4 * lo + i % 4, 4 * hi, 4)
-            if qs[i] == "v":
-                ts(h, o, 0.0625, None, Alu.mult)
-            else:
-                act(h, o, Act.Copy, scale=0.0625)
+        x0 = max(0, min(lo, hi - 128))
+        n = max(hi, x0 + 128) - x0
+        buf, k = banks[e].pop(0)
+        banks[e].append((buf, k))
+        mm((buf, k), "ab"[i // 4], 128 * (i % 4), q, C[t] + x0, n)
+        o = V(buf, 512 * k + lo - x0, 512 * k + hi - x0)
+        h = V("h%s%d" % ("ab"[i // 4], t), 4 * lo + i % 4, 4 * hi, 4)
+        if e == "v":
+            ts(h, o, 0.0625, None, Alu.mult)
+        else:
+            act(h, o, Act.Copy, scale=0.0625)
 
-    def kidq(t, pieces):
-        q, w = "r%d" % t, NW[t]
-        return [p and (lambda k=p[0], x=p[1], y=p[2]: quant(q, 2 * k * w + x, 2 * k * w + y, V("h%s%d" % ("ab"[k], t), 4 * x, 4 * y))) for p in pieces]
+    def kidq(t, k, x=0, y=None):
+        w = NW[t]
+        y = y or w
+        quant("r%d" % t, 2 * k * w + x, 2 * k * w + y, V("h%s%d" % ("ab"[k], t), 4 * x, 4 * y))
 
-    def fillin(jobs):
-        job = jobs.pop(0) if jobs else None
-        if job:
-            job()
-
-    def order(t, flight1, flight2, hook2, jobs):
-        chunks, back = plan[t]
+    def order(t, flight1, flight2, beside_mask, beside_list, late):
         lp = landpos(r, t)
         land, so, z = "land%d" % t, "so%d" % t, CMPW // 2
-        chunks_of = [[k for k, c in enumerate(CH[t]) if c[3] == s] for s in range(N)]
-        mine = chunks_of[r]
-        lo = CH[t][mine[0]][0] + 32 * CH[t][mine[0]][1]
-        hi = CH[t][mine[-1]][0] + 32 * CH[t][mine[-1]][2]
+        mine = chunks_of(t, r)
+        lo, hi = max(0, 128 * mine[0] + OFF[t]), 128 * mine[-1] + 128 + OFF[t]
         W = hi - lo
 
         def row(a, b):
@@ -334,97 +355,109 @@ def rank_program(g, core, T, topo):
         def part(k, m=1):
             return V(so, 9 * (z - 1) + k, 9 * (z - 1) + k + m, 9 if m == 1 else 1)
 
+        def signs(i, val):
+            act(V("sg%d" % t, 320 * i, 320 * i + W), V("pch", 1536, 1536 + W), Act.Sign, bias=val, scale=-1.0)
+
+        def ones(i, scale):
+            act(V("sj%d" % t, 320 * i, 320 * i + W), V("sg%d" % t, 320 * i, 320 * i + W), Act.Relu, scale=scale, accum=V("acc%d" % t, i, i + 1))
+
+        if len(mine) == 3:
+            signs(2, V("own%d" % t, 2, 3))
+            ones(2, 1.0)
         for i, k in enumerate(mine):
-            s = CH[t][k][0]
-            e = s + 128
+            e = 128 * k + 128 + OFF[t]
+            s = max(0, e - 128)
             val = V("own%d" % t, i, i + 1)
             x = CMPW * k
-            q = V("eq%d" % t, 128 * i, 128 * i + 128)
+            q = V("eq%d" % t, 128 * i, 128 * i + e - s)
             ts(q, row(s, e), val, None, Alu.is_equal)
+            if i == 2:
+                d = e - s + 1
+                scan(V("tif", 0, d), V("nid", 0, d), V("eq%d" % t, 128 * i, 128 * i + d), 0.0, Alu.mult, Alu.subtract)
+                act(part(k), V("acc%d" % t, i, i + 1), Act.Identity, scale=-1.0, bias=V("tif", d - 1, d))
+                continue
             ts(V("cmp%d" % t, x, x + e - lo), row(lo, e), val, None, Alu.is_ge)
-            scan(V("tie%d" % t, 128 * i, 128 * i + 128), V("nid"), q, 0.0, Alu.mult, Alu.subtract)
+            if i == 0:
+                flight1[0]()
+            scan(V("tie%d" % t, 128 * i + 128 - e + s, 128 * i + 128), V("nid", 128 - e + s, 128), q, 0.0, Alu.mult, Alu.subtract)
             if e < hi:
                 ts(V("cmp%d" % t, x + e - lo, x + W), row(e, hi), val, None, Alu.is_gt)
-        for i, k in enumerate(mine):
+        for i, k in enumerate(mine[:2]):
             total_of(k, W, V("tie%d" % t, 128 * i + 127, 128 * i + 128))
-        flight1()
-        first_r, second_r, third_r = sorted(others_r, key=lambda s: targets(T.cores[s]).index(core))
-        byS, byV = (third_r, second_r) if len(chunks_of[second_r]) > len(chunks_of[third_r]) else (second_r, third_r)
-        for i, k in enumerate(chunks_of[byS]):
-            act(V("sg%d" % t, 320 * i, 320 * i + W), V("pch", 1536, 1536 + W), Act.Sign, bias=V(land, lp[k], lp[k] + 1), scale=-1.0)
-        for i, k in enumerate(chunks_of[byS]):
-            act(V("sj%d" % t, 320 * i, 320 * i + W), V("sg%d" % t, 320 * i, 320 * i + W), Act.Relu, scale=1.0 if r < byS else -1.0, accum=V("acc%d" % t, i, i + 1))
-        n = len(chunks_of[byS])
-        act(part(chunks_of[byS][0], n), V("acc%d" % t, 0, n), Act.Copy, scale=-1.0 if r < byS else 1.0, bias=float(W) if r < byS else 0.0)
+        flight1[1]()
+        byS = senders[2] if len(chunks_of(t, senders[1])) > len(chunks_of(t, senders[2])) else senders[1]
+        cs = chunks_of(t, byS)
+        for i, k in enumerate(cs):
+            signs(i, V(land, lp[k], lp[k] + 1))
+        for i, k in enumerate(cs):
+            ones(i, 1.0 if r < byS else -1.0)
+        act(part(cs[0], len(cs)), V("acc%d" % t, 0, len(cs)), Act.Copy, scale=-1.0 if r < byS else 1.0, bias=float(W) if r < byS else 0.0)
         last = None
-        for s in (first_r, byV):
-            for k in chunks_of[s]:
+        for s in senders:
+            for k in chunks_of(t, s) if s != byS else []:
                 ts(V("cmp%d" % t, CMPW * k, CMPW * k + W), row(lo, hi), V(land, lp[k], lp[k] + 1), None, Alu.is_ge if r < s else Alu.is_gt)
                 if last is not None:
                     total_of(last, W)
                 last = k
         total_of(last, W)
-        for h in sorted(half, key=lambda h: core not in h):
-            cs = [c for c in others if c in h]
-            k0 = group(T.rank_of(h[0]), t)[0]
-            send([T["pland%d" % t][:, 5 * slot(T.rank_of(c), r):5 * slot(T.rank_of(c), r) + 5] for c in cs], part(k0, 5), cs, "cnt%d_%d" % (t, r))
-        k0, nc = chunks[0], len(chunks)
+        for cs in counted(r):
+            send([T["pland%d" % t][:, slot(T.rank_of(c), r):slot(T.rank_of(c), r) + 5] for c in cs], part(take(t, T.rank_of(cs[0])), 5), cs, "cnt%d_%d" % (t, r))
+        k0, nc = NEED[t][r]
+        srt = sorted(senders, key=lambda s: (sum(counted(s), []).index(core), not near(core, T.cores[s])))
+
+        def got(s, i=0, p0=0, p1=128):
+            x = slot(r, s) + k0 - take(t, r)
+            return V("pland%d" % t, x + i, x + nc, 1, p0, p1)
         flight2()
         at = V("rho%d" % t, 0, nc)
         ts(at, part(k0, nc), -1.0, float(K), Alu.mult, Alu.add)
-        o = chunks[0] - group(r, t)[0]
-        srt = sorted(others_r, key=lambda s: (s // 2 != r // 2, near(core, T.cores[s])))
         for i, s in enumerate(srt[:2]):
-            to = V("rho%d" % t, 5 * i + 5, 5 * i + 5 + nc)
-            tt(to, at, V("pland%d" % t, 5 * slot(r, s) + o, 5 * slot(r, s) + o + nc), Alu.subtract)
+            to = V("rho%d" % t, 8 * i + 8, 8 * i + 8 + nc)
+            tt(to, at, got(s), Alu.subtract)
             at = to
-        mq, g0, lo1, l0 = "mq%d" % t, CH[t][chunks[0]][0], WIN[t + 1][r][0], 5 * slot(r, srt[2]) + o
-        even = [k for k in chunks if CH[t][k][0] - g0 == 128 * (k - chunks[0])]
-
-        def mask(to, i, n, a):
-            tt(to, V("pland%d" % t, l0 + i, l0 + i + n, 1, 32 * a, 32 * a + 32), V("rho%d" % t, 10 + i, 10 + i + n, 1, 32 * a, 32 * a + 32), Alu.is_lt)
+        mq, lo1, g0 = "mq%d" % t, WIN[t + 1][r][0], 128 * k0 + OFF[t]
         for a in range(4):
-            mask(V(mq, 3 + a, 3 + 4 * len(even), 4, 0, 32), 0, len(even), a)
-        for k in chunks[len(even):]:
-            c = CH[t][k]
-            for a in range(c[1], c[2]):
-                x = 3 + (c[0] - g0) // 32 + a
-                mask(V(mq, x, x + 1, 1, 0, 32), k - chunks[0], 1, a)
-        hook2()
-        start = 0.0
-        if back:
-            start, x = V("tot%d" % t, 0, 1, 1, 0, 32), V(mq, 3, 3 + 4 * nc, 1, 0, 32)
-            op("v", lambda: g.vector.tensor_reduce(start[0], x[0], AxisListType.X, Alu.add, negate=True), [x], [start])
+            i = int(g0 + 32 * a < 0)
+            tt(V(mq, 3 + a + 4 * i, 3 + 4 * nc, 4, 0, 32), got(srt[2], i, 32 * a, 32 * a + 32), V("rho%d" % t, 16 + i, 16 + nc, 1, 32 * a, 32 * a + 32), Alu.is_lt)
+        beside_mask()
         nq = (NW[t + 1] + 16 * M - 1) // (16 * M)
         for a in range(nq):
             y = 3 + (lo1 + 16 * M * a - K - g0) // 32 + 5
-            n = y - min(2, y - 6)
-            scan(V("msp", B0 - 32 * (n - 6), B0 + FW, 32, 32 * a, 32 * a + 32), V("cz", 29 - n, 29, 1, 0, 32), V(mq, y - n, y, 1, 0, 32), start, Alu.mult, Alu.add)
-        fillin(jobs)
-        scan(V("mrep"), V("carb"), V("msp", B0), 0.0, Alu.mult, Alu.add)
-        fillin(jobs)
+            if sig > 0:
+                n = y - min(2, y - 6)
+                to, of = V("msp", B0 - 32 * (n - 6), B0 + FW, 32, 32 * a, 32 * a + 32), V(mq, y - n, y, 1, 0, 32)
+            else:
+                n = max(3 + 4 * nc - y, 1) + 5
+                to, of = back("msp", 0, 32 * n, 32, 32 * a, 32 * a + 32), back(mq, y - 5, y - 5 + n, 1, 0, 32)
+            scan(to, V("cz", 29 - n, 29, 1, 0, 32), of, 0.0, Alu.mult, Alu.add)
+        scan(V("mrep"), V("carb"), V("msp", m0, m0 + FW), 0.0, Alu.mult, Alu.add)
         turn(V("mrow%d" % t), V("mrep"))
-        fillin(jobs)
         fb = "fb%d" % t
-        scan(V(fb), V("mrow%d" % t), V("inc"), 0.0 if back else -float(K), Alu.add, Alu.add)
-        fillin(jobs)
-        for i in range(M):
-            ts(V("ch", CW * i, CW * i + SW), V(fb, 31 + 16 * i, 31 + 16 * i + SW), V("jt", M + i, M + i + 1), V("jt", 2 * M + i, 2 * M + i + 1), Alu.max, Alu.min)
-        scan(V("cu"), V("car2"), V("ch"), 0.0, Alu.mult, Alu.add)
-        fillin(jobs)
-        fillin(jobs)
-        sm, W = V("cu", CW - 1, M * CW, CW), NW[t]
-        ts(V("qi%d" % t), sm, -1.0 / 3, None, Alu.mult)
-        ts(V("ws%d" % t), sm, -float(W), V("xc%d" % t), Alu.mult, Alu.add)
-        ts(V("wy%d" % t), V("qi%d" % t), float(1 - 3 * W), None, Alu.mult)
-        fillin(jobs)
+        if sig > 0:
+            scan(V(fb), V("mrow%d" % t), V("inc"), -float(K), Alu.add, Alu.add)
+        else:
+            scan(back(fb, 0, FW), back("mrow%d" % t, 0, FW), V("inc"), 32.0 - FW, Alu.add, Alu.add)
+        f0 = 31 if sig > 0 else 0
+        for i in range(2):
+            act(V("sj2%d" % t, 96 * i, 96 * i + SW), V(fb, f0 + 16 * MV, f0 + 16 * MV + SW), Act.Relu, bias=V("jb", 2 * M + i, 2 * M + i + 1), accum=V("ac2%d" % t, i, i + 1))
+        act(V("cu", M * CW - 1, M * CW), V("ac2%d" % t, 1, 2), Act.Identity, scale=-1.0, bias=V("ac2%d" % t, 0, 1))
+        for i in range(MV):
+            ts(V("ch", CW * i, CW * i + SW), V(fb, f0 + 16 * i, f0 + 16 * i + SW), V("jb", i, i + 1), V("jb", M + i, M + i + 1), Alu.max, Alu.min)
+        scan(V("cu", 0, MV * CW), V("car2"), V("ch", 0, MV * CW), 0.0, Alu.mult, Alu.add)
+        if late:
+            kidq(t, 1, 0, NW[t] // 2)
+        sm, x = V("cu", CW - 1, M * CW, CW), 4 * M * t
+        ts(V("tri", x, x + 4 * M, 4), sm, -sig / 3, BIG, Alu.mult, Alu.add)
+        act(V("tri", x + 2, x + 4 * M, 4), sm, Act.Identity, scale=-sig * NW[t], bias=V("xc%d" % t))
+        beside_list()
+        if late:
+            kidq(t, 1, NW[t] // 2, NW[t])
         n = NW[t + 1] // 16
         for a in range(nq):
-            tt(V("wf%d" % t, M * a, M * a + M, 1, 0, 32), V("ws%d" % t, 0, M, 1, 32 * a, 32 * a + 32), V("wy%d" % t, 0, M, 1, 32 * a, 32 * a + 32), Alu.add)
-        while jobs:
-            fillin(jobs)
+            scan(V("wf%d" % t, 4 * M * a, 4 * M * a + 4 * M, 1, 0, 32), V("trd", x, x + 4 * M, 1, 32 * a, 32 * a + 32), V("tri", x, x + 4 * M, 1, 32 * a, 32 * a + 32),
+                 0.0, Alu.mult, Alu.add)
         for b in range(4):
-            copy("v", V("wu%d" % t, 0, n, 1, 32 * b, 32 * b + 32), V("wf%d" % t, 0, n, 1, 0, 32))
+            copy("v", V("wu%d" % t, 0, n, 1, 32 * b, 32 * b + 32), V("wf%d" % t, 3, 4 * n, 4, 0, 32))
 
     def pick(t, x=0, y=None):
         y, w = y or NW[t + 1], 3 * NW[t]
@@ -439,68 +472,79 @@ def rank_program(g, core, T, topo):
         off, a = V("wu%d" % t, 0, n // 16), V("tn%d" % t, 0, w)
         op("s", lambda: g.scalar.activation(out[0], a[0].indirect(off[0]), Act.Copy), [a, off], [out])
 
-    border = [(0, own0[0])] * (own0[0] > 0) + [(own0[1], NW[0])] * (own0[1] < NW[0])
-    if len(border) == 2:
-        jobs = [(0, 144, 288), None, None, None, None, (1, 0, NW[0]), (0, 0, 144), (0, 288, NW[0])]
-    elif r == 0:
-        jobs = [(0, 0, 144), None, None, None, None, (1, 0, NW[0]), (0, 144, NW[0])]
-    else:
-        jobs = [(0, 144, NW[0]), None, None, None, None, (1, 0, NW[0]), (0, 0, 144)]
-    inner = jobs.pop(0)
+    def nothing():
+        pass
 
-    def flight_of_scores0():
+    def first_own():
         quant("a", 0, 512, V("at"))
+        for i in range(2):
+            kid(0, i, "s", own0)
+
+    def second_tiles():
+        quant("b", 0, 512, V("bt"))
+        if short:
+            quant("r1", NW[1] - 128, NW[1], V("xt", 0, 512))
 
     def flight_of_counts0():
-        kids(0, "vsvsssss", range(4), own0)
-        quant("b", 0, 512, V("bt"))
-        kidq(0, [inner])[0]()
-        kids(0, "ssssssss", range(4, 5), own0)
+        for i in range(2, 4):
+            kid(0, i, "s", own0)
+        for x in right:
+            for i in range(4):
+                kid(0, i, "v", x)
+        kidq(0, 0, own0[0], NW[0])
+        for i in range(4, 8):
+            kid(0, i, "s")
         for i in range(3):
-            op("g", lambda: g.iota(T.tn0[:, NW[0] * i:NW[0] * i + NW[0]], [[4, NW[0]]], 4 * WIN[0][r][0] + (2 if i == 2 else 0), 0, allow_small_or_imprecise_dtypes=True),
-               [], [V("tn0", NW[0] * i, NW[0] * i + NW[0])])
+            count(V("tn0", NW[0] * i, NW[0] * i + NW[0]), 4, 4 * WIN[0][r][0] + (2 if i == 2 else 0))
 
-    def rest_kids():
-        kids(0, "ssssssss", range(5, 8))
-        for x in border:
-            kids(0, "ssssssss", range(4, 5), x)
-        for x in border:
-            kids(0, "ssssssss", range(4), x)
-    order(0, flight_of_scores0, flight_of_counts0, rest_kids, kidq(0, jobs))
-    mine1 = [c for c in CH[1] if c[3] == r]
-    o0, o1 = mine1[0][0] - WIN[1][r][0], mine1[-1][0] + 128 - WIN[1][r][0]
-    pick(0, o0, o0 + 128)
-    pick(0, o0 + 128, o1)
+    def first_left():
+        for x in left:
+            for i in range(4):
+                kid(0, i, "s", x)
+    order(0, [first_own, second_tiles], flight_of_counts0, nothing, first_left, True)
+    mine1 = chunks_of(1, r)
+    ends = [max(0, 128 * k + OFF[1]) - WIN[1][r][0] for k in mine1 + [mine1[-1] + 1]]
+    for x, y in zip(ends, ends[1:]):
+        pick(0, x, y)
     score(1)
-    for x, y in ((0, o0), (o1, NW[1])):
+    if left:
+        kidq(0, 0, 0, 128)
+    for x, y in ((0, ends[0]), (ends[-1], NW[1])):
         if y > x:
             pick(0, x, y)
-    bank[0] = 0
+    banks["s"] = banks["v"] = [("pch", 0), ("pch", 1), ("pch", 2), ("psc", 1), ("psc", 2), ("psc", 3)]
+    n1, who, first = ((1, "ssvsvsss", 5), (2, "ssvsvsss", 5), (2, "ssvsvsss", 5), (3, "sssvsvss", 4))[r]
 
     def flight_of_scores1():
-        kids(1, "ss", range(2))
-        quant("w", 0, 128, V("wt"))
+        for i in range(n1):
+            kid(1, i, "s")
 
     def flight_of_counts1():
-        kids(1, "ssssvsvs", range(2, 8))
-        for job in kidq(1, [(0, 0, NW[1]), (1, 0, NW[1])]):
-            job()
+        quant("w", 0, 128, V("wt"))
+        for i in range(n1, 8):
+            if i == first:
+                kidq(1, 0)
+            kid(1, i, who[i])
+        if not right:
+            kidq(1, 1)
 
     def new_numbers():
         numbers(0, V("tn1", 0, NW[1]))
         copy("s", V("tn1", NW[1], 2 * NW[1]), V("tn1", 0, NW[1]))
+
+    def second_numbers():
         act(V("tn1", 2 * NW[1], 3 * NW[1]), V("tn1", 0, NW[1]), Act.Identity, bias=1.0)
-    order(1, flight_of_scores1, flight_of_counts1, new_numbers, [])
+    order(1, [flight_of_scores1, nothing], flight_of_counts1, new_numbers, second_numbers, bool(right))
     cut = ((0, 160), (160, E))
     for x, y in cut:
         pick(1, x, y)
     outs = [mm(("psc", i), "w", 0, "r2", x, y - x) for i, (x, y) in enumerate(cut)]
-    for k in range(4):
-        dma("s", T.osc[4 * k:4 * k + 4, :], T.r2s[32 * k:32 * k + 4, :], "out", [V("r2s")], [])
     numbers(1, V("hsr"))
+    dma("s", T.hs[:], T.hsr[0:1, :], "out", [V("hsr")], [])
     for x, y in cut:
         dma("y", T.oc[:, 4 * x:4 * y], codes("r2c", x, y), "out", [V("r2c", x, y)], [])
-    dma("s", T.hs[:], T.hsr[0:1, :], "out", [V("hsr")], [])
+    for k in range(4):
+        dma("y", T.osc[4 * k:4 * k + 4, :], T.r2s[32 * k:32 * k + 4, :], "out", [V("r2s")], [])
     for o, (x, y) in zip(outs, cut):
         copy("v", V("ysb", x, y), o)
         dma("y", T.y[:, x:y], T.ysb[:, x:y], "out", [V("ysb", x, y)], [])

from concourse.bass import DstId, RemoteDMATransfer
from concourse.mybir import dt, AluOpType as Alu, ActivationFunctionType as Act

N, P, K, E = 4, 256, 64, 288
OWNER = ([0, 0, 1, 1, 2, 2, 3, 3], [0, 0, 0, 1, 1, 2, 2, 3, 3])
OFF = (0, -64)
NEED = ([(0, 3), (0, 5), (3, 5), (5, 3)], [(0, 3), (0, 5), (4, 5), (6, 3)])
WIN = ([(0, 320), (160, 576), (448, 864), (736, 1024)], [(0, 320), (224, 576), (512, 864), (800, 1088)], [(E * r, E * r + E) for r in range(N)])
F32, BF, I32, U16 = "float32", "bfloat16", "int32", "uint16"
M = 6
MV = 5
SW = 81
CW = 84
FW = 192
B0 = 512
CMPW = 448
BIG = 1.5 * 2 ** 23

SCRATCH = {
    "xt": ("sbuf", [128, 1024], BF), "u0": ("sbuf", [128, 512], BF), "ut": ("sbuf", [128, 512], BF),
    "uz": ("sbuf", [128, 192], BF), "one": ("sbuf", [128, 136], BF), "nid": ("sbuf", [128, 136], BF),
    "at": ("sbuf", [128, 2048], BF), "bt": ("sbuf", [128, 2048], BF), "wt": ("sbuf", [128, 512], BF),
    "msp": ("sbuf", [128, B0 + FW], BF), "mrep": ("sbuf", [128, FW], BF), "carb": ("sbuf", [128, FW], BF), "inc": ("sbuf", [128, FW], BF),
    "cz": ("sbuf", [128, 32], BF), "jt": ("sbuf", [128, 2 * M], F32), "jb": ("sbuf", [128, 2 * M + 2], F32), "ch": ("sbuf", [128, M * CW], BF),
    "cu": ("sbuf", [128, M * CW], BF), "car2": ("sbuf", [128, MV * CW], BF),
    "pi": ("sbuf", [128, 4], I32), "dcol": ("sbuf", [128, 4], F32),
    "psc": ("psum", [128, 2048], F32), "pch": ("psum", [128, 2048], F32),
    "tri": ("sbuf", [128, 8 * M], F32), "trd": ("sbuf", [128, 8 * M], F32), "tif": ("sbuf", [128, 132], F32),
    "ysb": ("sbuf", [128, 288], F32), "hsr": ("sbuf", [128, 288], F32),
    "tn0": ("sbuf", [128, 1248], F32), "tn1": ("sbuf", [128, 1056], F32),
}
for _q, _n in (("z", 128), ("u", 128), ("a", 512), ("b", 512), ("w", 128), ("r0", 1248), ("r1", 1056), ("r2", 288)):
    SCRATCH[_q + "c"] = ("sbuf", [128, _n], "float8_e4m3fn_x4")
    SCRATCH[_q + "s"] = ("sbuf", [128, _n], "uint8")
for _t in range(2):
    for _n, _w, _d in (("ha", 1664, BF), ("hb", 1664, BF), ("own", 4, F32), ("land", 8, F32), ("cmp", 9 * CMPW, BF),
                       ("eq", 392, BF), ("tie", 256, BF), ("sg", 3 * 320, BF), ("sj", 3 * 320, BF), ("so", 9 * CMPW // 2, BF), ("acc", 3, F32),
                       ("pland", 24, BF), ("rho", 24, BF), ("mrow", FW, BF), ("fb", FW, BF), ("mq", 32, BF), ("xc", 1, F32),
                       ("ac2", 2, F32), ("sj2", 192, BF), ("wf", 16 * M, F32), ("wu", 24, U16)):
        SCRATCH["%s%d" % (_n, _t)] = ("sbuf", [128, _w], _d)
SEMAPHORES = ["v", "s", "p", "gc", "sent", "arrl", "arrr", "dx0", "dx1", "du", "da", "db", "dw", "out"] + ["%s%d_%d" % (k, t, r) for k in ("arr", "cnt") for t in range(2) for r in range(N)]


def rank_program(g, core, T, topo):
    r = T.rank_of(core)
    if r is None:
        return
    Q = {"v": g.vector, "s": g.scalar, "p": g.tensor, "g": g, "y": g.sync}
    ESEM = {"v": "v", "s": "s", "p": "p", "g": "gc"}
    total, known, hist = {}, {q: {} for q in Q}, {}

    def V(name, c0=0, c1=None, step=1, p0=0, p1=128):
        if c1 is None:
            c1 = SCRATCH[name][1][1]
        ap = T[name][p0:p1, c0:c1] if step == 1 else T[name][p0:p1, c0:c1:step]
        return (ap, name, c0, c1, step, p0, p1)

    def back(name, c0, c1, step=1, p0=0, p1=128):
        last = c0 + (c1 - 1 - c0) // step * step
        return (T[name][p0:p1, last:(c0 - 1 if c0 else None):-step], name, c0, c1, step, p0, p1)

    def clash(x, y):
        if SCRATCH[x[1]][0] == "psum":
            return x[2] // 512 <= (y[3] - 1) // 512 and y[2] // 512 <= (x[3] - 1) // 512
        if x[6] <= y[5] or y[6] <= x[5] or x[3] <= y[2] or y[3] <= x[2]:
            return False
        return not set(range(x[2], x[3], x[4])).isdisjoint(range(y[2], y[3], y[4]))

    def need(q, reads, writes):
        todo = {}
        for acc, wr in [(a, False) for a in reads] + [(a, True) for a in writes]:
            psum = SCRATCH[acc[1]][0] == "psum"
            for old, owr, s, n, clock, oq in hist.get(acc[1], []):
                if not (wr or owr or (psum and oq != q)) or known[q].get(s, 0) >= n or not clash(acc, old):
                    continue
                if s not in todo or todo[s][0] < n:
                    todo[s] = (n, clock)
        for s in sorted(todo):
            n, clock = todo[s]
            if known[q].get(s, 0) < n:
                Q[q].wait_ge(T.sem[s], n)
                known[q][s] = n
                for s2, n2 in clock.items():
                    known[q][s2] = max(known[q].get(s2, 0), n2)

    def note(q, reads, writes, s, n):
        clock = dict(known[q])
        for acc, wr in [(a, False) for a in reads] + [(a, True) for a in writes]:
            hist.setdefault(acc[1], []).append((acc, wr, s, n, clock, q))

    def op(q, call, reads, writes):
        need(q, reads, writes)
        s = ESEM[q]
        total[s] = total.get(s, 0) + 1
        call().then_inc(T.sem[s], 1)
        note(q, reads, writes, s, total[s])

    def dma(q, out, in_, sem, reads, writes):
        need(q, reads, writes)
        total[sem] = total.get(sem, 0) + 16
        Q[q].dma_start(out, in_).then_inc(T.sem[sem], 16)
        note(q, reads, writes, sem, total[sem])

    def sc(x):
        return x[0] if isinstance(x, tuple) else x

    def ts(out, in0, s1, s2, op0, op1=None):
        rd = [x for x in (in0, s1, s2) if isinstance(x, tuple)]
        if op1 is None:
            op("v", lambda: g.vector.tensor_scalar(out[0], in0[0], sc(s1), None, op0), rd, [out])
        else:
            op("v", lambda: g.vector.tensor_scalar(out[0], in0[0], sc(s1), sc(s2), op0, op1), rd, [out])

    def tt(out, a, b, o):
        op("v", lambda: g.vector.tensor_tensor(out[0], a[0], b[0], o), [a, b], [out])

    def copy(q, out, in_):
        if q == "v":
            op("v", lambda: g.vector.tensor_copy(out[0], in_[0]), [in_], [out])
        else:
            op("s", lambda: g.scalar.activation(out[0], in_[0], Act.Copy), [in_], [out])

    def act(out, in_, f, bias=0.0, scale=1.0, accum=None):
        rd = [in_] + [x for x in (bias, scale) if isinstance(x, tuple)]
        if accum is None:
            op("s", lambda: g.scalar.activation(out[0], in_[0], f, bias=sc(bias), scale=sc(scale)), rd, [out])
        else:
            op("s", lambda: g.scalar.activation(out[0], in_[0], f, bias=sc(bias), scale=sc(scale), accum_out=accum[0]), rd, [out, accum])

    def scan(out, a, b, initial, o0, o1):
        rd = [x for x in (a, b, initial) if isinstance(x, tuple)]
        op("v", lambda: g.vector.tensor_tensor_scan(out[0], a[0], b[0], sc(initial), o0, o1), rd, [out])

    def turn(out, in_):
        op("v", lambda: g.vector.transpose(out[0], in_[0]), [in_], [out])

    def fill(out, c):
        op("v", lambda: g.vector.memset(out[0], c), [], [out])

    def count(out, step, base):
        n = len(range(out[2], out[3], out[4]))
        op("g", lambda: g.iota(out[0], [[step, n]], base, 0, allow_small_or_imprecise_dtypes=True), [], [out])

    def quant(q, a, b, in_):
        c, s = V(q + "c", a, b), V(q + "s", a, b)
        op("v", lambda: g.vector.quantize_mx(c[0], s[0], in_[0]), [in_], [c, s])

    def mm(bank, q1, a1, q2, a2, n):
        o = V(bank[0], 512 * bank[1], 512 * bank[1] + n)
        w, ws, x, xs = V(q1 + "c", a1, a1 + 128), V(q1 + "s", a1, a1 + 128), V(q2 + "c", a2, a2 + n), V(q2 + "s", a2, a2 + n)
        op("p", lambda: g.tensor.matmul_mx(o[0], w[0], ws[0], x[0], xs[0], True, True), [w, ws, x, xs], [o])
        return o

    def dst(c):
        rid, pid = topo.addr(c)[:2]
        return DstId(rid=rid, pnc=pid)

    def engines(cs):
        return sorted(set.intersection(*[set(topo.engines(core, c)) for c in cs]))

    def send(outs, src, cs, sem):
        e = engines(cs)
        need("g", [src], [])
        g.remote_dma_fused([RemoteDMATransfer(dst_ids=[dst(c) for c in cs], dma_engine_mask=sum(1 << k for k in e), remote_sem=T.sem[sem],
                                              srcs=[src[0]], dsts=outs)], local_sem=T.sem.sent)
        total["sent"] = total.get("sent", 0) + len(e)

    def arrive(sem, n, views):
        total[sem] = total.get(sem, 0) + n
        for v in views:
            hist.setdefault(v[1], []).append((v, True, sem, total[sem], {}, None))

    def codes(name, a, b):
        return T[name][:, a:b].bitcast(dt.uint8)

    def near(c, d):
        return topo.same_plane(topo.chip(c), topo.chip(d))

    def targets(c):
        i = T.rank_of(c)
        return sorted([d for d in T.cores if d != c], key=lambda d: (near(c, d), (T.rank_of(d) - i) % N))

    NW = [WIN[t][r][1] - WIN[t][r][0] for t in range(3)]
    C = (NW[0], NW[1], 0)
    others = targets(core)
    senders = sorted([T.rank_of(c) for c in others], key=lambda s: targets(T.cores[s]).index(core))
    ENG = len(engines(others))
    sig = 1.0 if r < N // 2 else -1.0

    def slot(me, s):
        return 8 * (s if s < me else s - 1)

    def take(t, me):
        return 0 if me < N // 2 else len(OWNER[t]) - 5

    def counted(s):
        cs = targets(T.cores[s])
        return [[c for c in cs if (T.rank_of(c) // 2 == s // 2) == same] for same in (True, False)]

    def landpos(me, t):
        return {k: i for i, k in enumerate([k for k, s in enumerate(OWNER[t]) if s != me])}

    def chunks_of(t, s):
        return [k for k, o in enumerate(OWNER[t]) if o == s]

    halves = (0, 1) if r else (1, 0)
    for i in halves:
        dma("y", T.xt[:, 512 * i:512 * i + 512], T.x[:, 512 * i:512 * i + 512], "dx%d" % i, [], [V("xt", 512 * i, 512 * i + 512)])
    dma("s", T.u0[:, 0:8], T.u[:, 0:8], "du", [], [V("u0", 0, 8)])
    dma("y", T.at[:], T.a[:], "da", [], [V("at")])
    dma("y", T.bt[:], T.b[:], "db", [], [V("bt")])

    own0 = (P * r - WIN[0][r][0], P * r - WIN[0][r][0] + P)
    nb = [s for s in (r - 1, r + 1) if 0 <= s < N]
    left, right = [(0, own0[0])] * (r > 0), [(own0[1], NW[0])] * (r < N - 1)
    for sem, side in (("arrl", left), ("arrr", right)):
        for a, b in side:
            arrive(sem, 2 * ENG, [V("r0c", C[0] + a, C[0] + b), V("r0s", C[0] + a, C[0] + b)])
    for t in range(2):
        for s in senders:
            cols = [landpos(r, t)[k] for k in chunks_of(t, s)]
            arrive("arr%d_%d" % (t, s), ENG, [V("land%d" % t, cols[0], cols[-1] + 1)])
            arrive("cnt%d_%d" % (t, s), ENG, [V("pland%d" % t, slot(r, s), slot(r, s) + 5)])
    x = landpos(r, 0)[chunks_of(0, senders[0])[0]]
    dma("y", T.wt[:], T.w[:], "dw", [V("land0", x, x + 1)], [V("wt")])

    fill(V("uz"), 0.0)
    fill(V("u0", 8), 0.0)
    op("g", lambda: g.iota(T.pi[:, 0:1], [[0, 1]], 0, 1), [], [V("pi", 0, 1)])
    count(V("jt", 0, M), 16, -1)
    op("v", lambda: g.vector.tensor_scalar(T.pi[:, 1:2], T.pi[:, 0:1], 96, None, Alu.bitwise_and), [V("pi", 0, 1)], [V("pi", 1, 2)])
    op("v", lambda: g.vector.tensor_scalar(T.pi[:, 2:3], T.pi[:, 0:1], 15, None, Alu.bitwise_and), [V("pi", 0, 1)], [V("pi", 2, 3)])
    fill(V("one"), 1.0)
    ts(V("dcol", 0, 1), V("pi", 2, 3), 1.0, None, Alu.mult)
    ts(V("dcol", 1, 2), V("pi", 1, 2), 16.0 * M / 32, None, Alu.mult)
    op("g", lambda: g.affine_select(T.nid[:], T.one[:], [[-1, 136]], Alu.not_equal, 0.0, 0, 1), [V("one")], [V("nid")])
    fill(V("car2"), 1.0)
    fill(V("inc", 0, 32), 0.0)
    fill(V("car2", 0, MV * CW, CW), 0.0)
    fill(V("cz", 0, 24), 1.0)
    fill(V("cz", 24, 32), 0.0)

    def put(out, c):
        act(out, V("uz", 0, len(range(out[2], out[3], out[4]))), Act.Identity, bias=c)
    m0 = B0 if sig > 0 else 0
    put(V("msp", m0, m0 + FW), 0.0)
    put(V("carb"), 1.0)
    put(V("inc", 32), 1.0)
    for t in range(2):
        put(V("mq%d" % t), 0.0)
    for k in range(4):
        put(V("ut", k, 512, 4), V("u0", k, k + 1))
    put(V("carb", 0, FW, 32), 0.0)
    act(V("jt", M, 2 * M), V("jt", 0, M), Act.Identity, bias=V("dcol", 0, 1))
    act(V("ch", SW, M * CW, CW), V("jt", 0, M), Act.Identity, bias=sig * (-3.0 - SW), scale=sig * (-3.0 - SW))
    act(V("jb", 0, M), V("jt", M, 2 * M), Act.Identity, scale=sig, bias=0.0 if sig > 0 else -3.0)
    act(V("dcol", 2, 3), V("dcol", 0, 1), Act.Identity, bias=sig * 64.0, scale=sig * -64.0)
    act(V("dcol", 3, 4), V("dcol", 0, 1), Act.Identity, bias=sig * (SW - 64.0), scale=sig * (64.0 - SW))
    act(V("jb", M, 2 * M), V("jb", 0, M), Act.Identity, bias=3.0)
    for i in range(2):
        put(V("ch", SW + 1 + i, M * CW, CW), V("dcol", 2 + i, 3 + i))
    act(V("jb", 2 * M, 2 * M + 2), V("jb", M - 1, 2 * M, M), Act.Identity, scale=-1.0)
    for t in range(2):
        act(V("xc%d" % t), V("dcol", 1, 2), Act.Identity, bias=float(WIN[t + 1][r][0] - K - WIN[t][r][0] + 80 + NW[t]))
    short = len(chunks_of(1, r)) == 3

    def border_to(s, plane):
        sw = WIN[0][s]
        lo, hi = max(P * r, sw[0]), min(P * r + P, sw[1])
        a, b = lo - WIN[0][r][0] + C[0], hi - WIN[0][r][0] + C[0]
        e = sw[1] - sw[0] - sw[0]
        c, d = lo + e, hi + e
        sem = "arrl" if r < s else "arrr"
        if plane:
            send([T.r0s[:, c:d]], V("r0s", a, b), [T.cores[s]], sem)
        else:
            send([codes("r0c", c, d)], (codes("r0c", a, b),) + V("r0c", a, b)[1:], [T.cores[s]], sem)

    for i in halves:
        quant("r0", C[0] + own0[0] + 128 * i, C[0] + own0[0] + 128 * i + 128, V("xt", 512 * i, 512 * i + 512))
        if i == halves[0]:
            border_to(nb[0], True)
            quant("z", 0, 128, V("u0"))

    def score(t):
        q = "r%d" % t
        w0 = WIN[t][r][0] - C[t]
        mine = chunks_of(t, r)
        n = len(mine)
        for i in (range(n) if t else halves):
            mm(("psc", 1 + i), q, 128 * mine[i] + OFF[t] - w0, "z", 0, 128)
        ow = V("own%d" % t, 0, n)
        copy("v", ow, V("psc", 512, 512 * n + 1, 512))
        outs = []
        for c in others:
            p = landpos(T.rank_of(c), t)[mine[0]]
            outs.append(T["land%d" % t][:, p:p + n])
        send(outs, ow, others, "arr%d_%d" % (t, r))
        if t == 0:
            quant("u", 0, 128, V("ut"))
        lo, hi = max(0, 128 * mine[0] + OFF[t]), 128 * mine[-1] + 128 + OFF[t]
        mm(("psc", 0), "u", 0, q, lo - w0, hi - lo)
        mm(("pch", 3), "u", 0, q, lo - w0, hi - lo)

    score(0)
    for s in nb:
        border_to(s, False)
        if s != nb[0]:
            border_to(s, True)
    count(V("tri", 1, 8 * M, 4), 0, -int(BIG))
    count(V("tri", 3, 8 * M, 4), 0, 0)
    count(V("trd", 0, 8 * M, 4), 0, 0)
    count(V("trd", 1, 8 * M, 2), 0, 1)
    for t in range(2):
        count(V("trd", 4 * M * t + 2, 4 * M * t + 4 * M, 4), 0, 1 - 3 * NW[t])
    count(V("tri", 4 * M - 1, 8 * M, 4 * M), 0, 16 * MV if sig > 0 else -1)
    if short:
        count(V("eq1", 384, 386), 0, -NW[1])
    banks = {"s": [("pch", 0), ("pch", 1), ("pch", 2), ("psc", 1), ("psc", 2)], "v": [("psc", 3), ("psc", 0)]}

    def kid(t, i, e, cols=None):
        q, w = "r%d" % t, NW[t]
        lo, hi = cols or (0, w)
        x0 = max(0, min(lo, hi - 128))
        n = max(hi, x0 + 128) - x0
        buf, k = banks[e].pop(0)
        banks[e].append((buf, k))
        mm((buf, k), "ab"[i // 4], 128 * (i % 4), q, C[t] + x0, n)
        o = V(buf, 512 * k + lo - x0, 512 * k + hi - x0)
        h = V("h%s%d" % ("ab"[i // 4], t), 4 * lo + i % 4, 4 * hi, 4)
        if e == "v":
            ts(h, o, 0.0625, None, Alu.mult)
        else:
            act(h, o, Act.Copy, scale=0.0625)

    def kidq(t, k, x=0, y=None):
        w = NW[t]
        y = y or w
        quant("r%d" % t, 2 * k * w + x, 2 * k * w + y, V("h%s%d" % ("ab"[k], t), 4 * x, 4 * y))

    def order(t, flight1, flight2, beside_mask, beside_list, late):
        lp = landpos(r, t)
        land, so, z = "land%d" % t, "so%d" % t, CMPW // 2
        mine = chunks_of(t, r)
        lo, hi = max(0, 128 * mine[0] + OFF[t]), 128 * mine[-1] + 128 + OFF[t]
        W = hi - lo

        def row(a, b):
            return V("psc", a - lo, b - lo)

        def total_of(k, w, start=0.0):
            x, y = CMPW * k, w // 2
            scan(V(so, 9 * (z - y) + k, 9 * (z - 1) + k + 1, 9), V("cmp%d" % t, x, x + y), V("cmp%d" % t, x + y, x + w), start, Alu.add, Alu.add)

        def part(k, m=1):
            return V(so, 9 * (z - 1) + k, 9 * (z - 1) + k + m, 9 if m == 1 else 1)

        def signs(i, val):
            act(V("sg%d" % t, 320 * i, 320 * i + W), V("pch", 1536, 1536 + W), Act.Sign, bias=val, scale=-1.0)

        def ones(i, scale):
            act(V("sj%d" % t, 320 * i, 320 * i + W), V("sg%d" % t, 320 * i, 320 * i + W), Act.Relu, scale=scale, accum=V("acc%d" % t, i, i + 1))

        if len(mine) == 3:
            signs(2, V("own%d" % t, 2, 3))
            ones(2, 1.0)
        for i, k in enumerate(mine):
            e = 128 * k + 128 + OFF[t]
            s = max(0, e - 128)
            val = V("own%d" % t, i, i + 1)
            x = CMPW * k
            q = V("eq%d" % t, 128 * i, 128 * i + e - s)
            ts(q, row(s, e), val, None, Alu.is_equal)
            if i == 2:
                d = e - s + 1
                scan(V("tif", 0, d), V("nid", 0, d), V("eq%d" % t, 128 * i, 128 * i + d), 0.0, Alu.mult, Alu.subtract)
                act(part(k), V("acc%d" % t, i, i + 1), Act.Identity, scale=-1.0, bias=V("tif", d - 1, d))
                continue
            ts(V("cmp%d" % t, x, x + e - lo), row(lo, e), val, None, Alu.is_ge)
            if i == 0:
                flight1[0]()
            scan(V("tie%d" % t, 128 * i + 128 - e + s, 128 * i + 128), V("nid", 128 - e + s, 128), q, 0.0, Alu.mult, Alu.subtract)
            if e < hi:
                ts(V("cmp%d" % t, x + e - lo, x + W), row(e, hi), val, None, Alu.is_gt)
        for i, k in enumerate(mine[:2]):
            total_of(k, W, V("tie%d" % t, 128 * i + 127, 128 * i + 128))
        flight1[1]()
        byS = senders[2] if len(chunks_of(t, senders[1])) > len(chunks_of(t, senders[2])) else senders[1]
        cs = chunks_of(t, byS)
        for i, k in enumerate(cs):
            signs(i, V(land, lp[k], lp[k] + 1))
        for i, k in enumerate(cs):
            ones(i, 1.0 if r < byS else -1.0)
        act(part(cs[0], len(cs)), V("acc%d" % t, 0, len(cs)), Act.Copy, scale=-1.0 if r < byS else 1.0, bias=float(W) if r < byS else 0.0)
        last = None
        for s in senders:
            for k in chunks_of(t, s) if s != byS else []:
                ts(V("cmp%d" % t, CMPW * k, CMPW * k + W), row(lo, hi), V(land, lp[k], lp[k] + 1), None, Alu.is_ge if r < s else Alu.is_gt)
                if last is not None:
                    total_of(last, W)
                last = k
        total_of(last, W)
        for cs in counted(r):
            send([T["pland%d" % t][:, slot(T.rank_of(c), r):slot(T.rank_of(c), r) + 5] for c in cs], part(take(t, T.rank_of(cs[0])), 5), cs, "cnt%d_%d" % (t, r))
        k0, nc = NEED[t][r]
        srt = sorted(senders, key=lambda s: (sum(counted(s), []).index(core), not near(core, T.cores[s])))

        def got(s, i=0, p0=0, p1=128):
            x = slot(r, s) + k0 - take(t, r)
            return V("pland%d" % t, x + i, x + nc, 1, p0, p1)
        flight2()
        at = V("rho%d" % t, 0, nc)
        ts(at, part(k0, nc), -1.0, float(K), Alu.mult, Alu.add)
        for i, s in enumerate(srt[:2]):
            to = V("rho%d" % t, 8 * i + 8, 8 * i + 8 + nc)
            tt(to, at, got(s), Alu.subtract)
            at = to
        mq, lo1, g0 = "mq%d" % t, WIN[t + 1][r][0], 128 * k0 + OFF[t]
        for a in range(4):
            i = int(g0 + 32 * a < 0)
            tt(V(mq, 3 + a + 4 * i, 3 + 4 * nc, 4, 0, 32), got(srt[2], i, 32 * a, 32 * a + 32), V("rho%d" % t, 16 + i, 16 + nc, 1, 32 * a, 32 * a + 32), Alu.is_lt)
        beside_mask()
        nq = (NW[t + 1] + 16 * M - 1) // (16 * M)
        for a in range(nq):
            y = 3 + (lo1 + 16 * M * a - K - g0) // 32 + 5
            if sig > 0:
                n = y - min(2, y - 6)
                to, of = V("msp", B0 - 32 * (n - 6), B0 + FW, 32, 32 * a, 32 * a + 32), V(mq, y - n, y, 1, 0, 32)
            else:
                n = max(3 + 4 * nc - y, 1) + 5
                to, of = back("msp", 0, 32 * n, 32, 32 * a, 32 * a + 32), back(mq, y - 5, y - 5 + n, 1, 0, 32)
            scan(to, V("cz", 29 - n, 29, 1, 0, 32), of, 0.0, Alu.mult, Alu.add)
        scan(V("mrep"), V("carb"), V("msp", m0, m0 + FW), 0.0, Alu.mult, Alu.add)
        turn(V("mrow%d" % t), V("mrep"))
        fb = "fb%d" % t
        if sig > 0:
            scan(V(fb), V("mrow%d" % t), V("inc"), -float(K), Alu.add, Alu.add)
        else:
            scan(back(fb, 0, FW), back("mrow%d" % t, 0, FW), V("inc"), 32.0 - FW, Alu.add, Alu.add)
        f0 = 31 if sig > 0 else 0
        for i in range(2):
            act(V("sj2%d" % t, 96 * i, 96 * i + SW), V(fb, f0 + 16 * MV, f0 + 16 * MV + SW), Act.Relu, bias=V("jb", 2 * M + i, 2 * M + i + 1), accum=V("ac2%d" % t, i, i + 1))
        act(V("cu", M * CW - 1, M * CW), V("ac2%d" % t, 1, 2), Act.Identity, scale=-1.0, bias=V("ac2%d" % t, 0, 1))
        for i in range(MV):
            ts(V("ch", CW * i, CW * i + SW), V(fb, f0 + 16 * i, f0 + 16 * i + SW), V("jb", i, i + 1), V("jb", M + i, M + i + 1), Alu.max, Alu.min)
        scan(V("cu", 0, MV * CW), V("car2"), V("ch", 0, MV * CW), 0.0, Alu.mult, Alu.add)
        if late:
            kidq(t, 1, 0, NW[t] // 2)
        sm, x = V("cu", CW - 1, M * CW, CW), 4 * M * t
        ts(V("tri", x, x + 4 * M, 4), sm, -sig / 3, BIG, Alu.mult, Alu.add)
        act(V("tri", x + 2, x + 4 * M, 4), sm, Act.Identity, scale=-sig * NW[t], bias=V("xc%d" % t))
        beside_list()
        if late:
            kidq(t, 1, NW[t] // 2, NW[t])
        n = NW[t + 1] // 16
        for a in range(nq):
            scan(V("wf%d" % t, 4 * M * a, 4 * M * a + 4 * M, 1, 0, 32), V("trd", x, x + 4 * M, 1, 32 * a, 32 * a + 32), V("tri", x, x + 4 * M, 1, 32 * a, 32 * a + 32),
                 0.0, Alu.mult, Alu.add)
        for b in range(4):
            copy("v", V("wu%d" % t, 0, n, 1, 32 * b, 32 * b + 32), V("wf%d" % t, 3, 4 * n, 4, 0, 32))

    def pick(t, x=0, y=None):
        y, w = y or NW[t + 1], 3 * NW[t]
        off = V("wu%d" % t, x // 16, y // 16)
        a, b = V("r%dc" % t, 0, w), V("r%dc" % (t + 1), C[t + 1] + x, C[t + 1] + y)
        op("v", lambda: g.vector.tensor_copy(b[0].bitcast(dt.uint32), a[0].bitcast(dt.uint32).indirect(off[0])), [a, off], [b])
        c, d = V("r%ds" % t, 0, w), V("r%ds" % (t + 1), C[t + 1] + x, C[t + 1] + y)
        op("s", lambda: g.scalar.activation(d[0], c[0].indirect(off[0]), Act.Copy), [c, off], [d])

    def numbers(t, out):
        n, w = NW[t + 1], 3 * NW[t]
        off, a = V("wu%d" % t, 0, n // 16), V("tn%d" % t, 0, w)
        op("s", lambda: g.scalar.activation(out[0], a[0].indirect(off[0]), Act.Copy), [a, off], [out])

    def nothing():
        pass

    def first_own():
        quant("a", 0, 512, V("at"))
        for i in range(2):
            kid(0, i, "s", own0)

    def second_tiles():
        quant("b", 0, 512, V("bt"))
        if short:
            quant("r1", NW[1] - 128, NW[1], V("xt", 0, 512))

    def flight_of_counts0():
        for i in range(2, 4):
            kid(0, i, "s", own0)
        for x in right:
            for i in range(4):
                kid(0, i, "v", x)
        kidq(0, 0, own0[0], NW[0])
        for i in range(4, 8):
            kid(0, i, "s")
        for i in range(3):
            count(V("tn0", NW[0] * i, NW[0] * i + NW[0]), 4, 4 * WIN[0][r][0] + (2 if i == 2 else 0))

    def first_left():
        for x in left:
            for i in range(4):
                kid(0, i, "s", x)
    order(0, [first_own, second_tiles], flight_of_counts0, nothing, first_left, True)
    mine1 = chunks_of(1, r)
    ends = [max(0, 128 * k + OFF[1]) - WIN[1][r][0] for k in mine1 + [mine1[-1] + 1]]
    for x, y in zip(ends, ends[1:]):
        pick(0, x, y)
    score(1)
    if left:
        kidq(0, 0, 0, 128)
    for x, y in ((0, ends[0]), (ends[-1], NW[1])):
        if y > x:
            pick(0, x, y)
    banks["s"] = banks["v"] = [("pch", 0), ("pch", 1), ("pch", 2), ("psc", 1), ("psc", 2), ("psc", 3)]
    n1, who, first = ((1, "ssvsvsss", 5), (2, "ssvsvsss", 5), (2, "ssvsvsss", 5), (3, "sssvsvss", 4))[r]

    def flight_of_scores1():
        for i in range(n1):
            kid(1, i, "s")

    def flight_of_counts1():
        quant("w", 0, 128, V("wt"))
        for i in range(n1, 8):
            if i == first:
                kidq(1, 0)
            kid(1, i, who[i])
        if not right:
            kidq(1, 1)

    def new_numbers():
        numbers(0, V("tn1", 0, NW[1]))
        copy("s", V("tn1", NW[1], 2 * NW[1]), V("tn1", 0, NW[1]))

    def second_numbers():
        act(V("tn1", 2 * NW[1], 3 * NW[1]), V("tn1", 0, NW[1]), Act.Identity, bias=1.0)
    order(1, [flight_of_scores1, nothing], flight_of_counts1, new_numbers, second_numbers, bool(right))
    cut = ((0, 160), (160, E))
    for x, y in cut:
        pick(1, x, y)
    outs = [mm(("psc", i), "w", 0, "r2", x, y - x) for i, (x, y) in enumerate(cut)]
    numbers(1, V("hsr"))
    dma("s", T.hs[:], T.hsr[0:1, :], "out", [V("hsr")], [])
    for x, y in cut:
        dma("y", T.oc[:, 4 * x:4 * y], codes("r2c", x, y), "out", [V("r2c", x, y)], [])
    for k in range(4):
        dma("y", T.osc[4 * k:4 * k + 4, :], T.r2s[32 * k:32 * k + 4, :], "out", [V("r2s")], [])
    for o, (x, y) in zip(outs, cut):
        copy("v", V("ysb", x, y), o)
        dma("y", T.y[:, x:y], T.ysb[:, x:y], "out", [V("ysb", x, y)], [])
    for s in sorted(total):
        if known["g"].get(s, 0) < total[s]:
            g.wait_ge(T.sem[s], total[s])
